import numpy as np
import ml_dtypes


def mxq(x, axis, fmt="e4m3"):
    dtype, down = {"e4m3": (ml_dtypes.float8_e4m3fn, 7), "e5m2": (ml_dtypes.float8_e5m2, 14)}[fmt]
    v = np.moveaxis(np.asarray(x, np.float32).astype(ml_dtypes.bfloat16).astype(np.float64), axis, -1)
    blocks = v.reshape(v.shape[:-1] + (-1, 32))
    amax = np.abs(blocks).max(-1, keepdims=True)
    byte = np.maximum(np.where(amax > 0, np.frexp(amax)[1] - 1 + 127, 0) - down, 1)
    scale = np.exp2(byte - 127.0)
    codes = (blocks / scale).astype(np.float32).astype(dtype).astype(np.float64)
    return np.moveaxis((codes * scale).reshape(v.shape), -1, axis)


WIDE = False


def mx_kscale(k):
    if not WIDE:
        return np.ones(k)
    levels = np.array([10, -10, 5, -5, 0])
    if k % 512:
        return np.exp2(np.random.permutation(np.resize(levels, k // 32))).repeat(32)
    a = np.empty((k // 512, 16))
    for p in range(k // 512):
        a[p, :8] = np.random.permutation(np.resize(levels, 8))
        for g in range(8):
            far = levels[np.abs(levels - a[p, g]) >= 10]
            a[p, g + 8] = far[np.random.randint(len(far))]
    return np.exp2(a.ravel()).repeat(32)


BF16 = ml_dtypes.bfloat16


def bf(x):
    return np.asarray(x, np.float32).astype(BF16)


def f64(x):
    return np.asarray(x).astype(np.float64)


B, D, R = 2048, 1024, 512


def setup_inputs():
    s = mx_kscale(D)
    q = mx_kscale(D)
    t = mx_kscale(B)
    return {"x": bf(np.random.standard_normal((B, D)) * s),
            "x0": bf(np.random.standard_normal((B, D)) * q),
            "dy": bf(np.random.standard_normal((B, D)) * t[:, None]),
            "v": bf(np.random.standard_normal((D, R)) / np.sqrt(D) / s[:, None]),
            "um": bf(np.random.standard_normal((D, R)) / np.sqrt(D) / q[:, None]),
            "a": bf(0.4 * np.random.standard_normal(R)),
            "omega": bf(np.random.uniform(0.5, 1.5, B) / np.sqrt(B) / t),
            "rv": bf(np.random.uniform(0.5, 1.5, D) / s),
            "ru": bf(np.random.uniform(0.5, 1.5, D) / q)}


def reference(x, x0, dy, v, um, a, omega, rv, ru):
    x, w = f64(x), f64(omega)[:, None]
    pre = mxq(x, 1, "e4m3") @ mxq(f64(v), 0, "e4m3")
    h = np.tanh(pre + f64(a))
    dz = f64(x0) * f64(dy)
    dh = mxq(dz, 1, "e4m3") @ mxq(f64(um), 0, "e4m3")
    dpre = dh * (1.0 - h * h)
    hw = w * h
    xw = w * x
    du = mxq(dz, 0, "e4m3").T @ mxq(hw, 0, "e4m3")
    dv = mxq(xw, 0, "e4m3").T @ mxq(dpre, 0, "e4m3")
    return f64(rv)[:, None] * dv, f64(ru)[:, None] * du

@@ -1,0 +1,405 @@
+from contextlib import ExitStack
+
+import concourse.mybir as mybir
+from concourse.masks import make_identity
+
+B, D, R = 2048, 1024, 512
+FLOPS = 4 * 2 * B * D * R
+
+F32 = mybir.dt.float32
+BF16 = mybir.dt.bfloat16
+U32 = mybir.dt.uint32
+U8 = mybir.dt.uint8
+FP8X4 = mybir.dt.float8_e4m3fn_x4
+ALU = mybir.AluOpType
+ACT = mybir.ActivationFunctionType
+
+P = 128
+GROUPS = 4
+NH = 5
+NIL = 4
+XB = (0, 7)
+ZB = (1,)
+PB = (2,)
+HB = (3,)
+DB = (5, 6)
+SWEEP_BANKS = ((0, 7, 1, 4), (2, 3, 5, 6))
+S_STEADY = 1
+S_RAMP = 2
+V_RAMP = 0
+RAMP = 12
+EARLY = 13
+V_TAIL = 2
+S_TAIL = 1
+E_TAIL = "S"
+PL = 1
+HEAD_PRE = 4
+HEAD_S = 3
+
+
+def tile_low_rank_cross_gradients_f4_kernel(tc, x, x0, dy, v, um, a, omega, rv, ru, out_0, out_1):
+    nc = tc.nc
+    with ExitStack() as ctx:
+        sb = ctx.enter_context(tc.tile_pool(name="sb", bufs=1))
+        ps = ctx.enter_context(tc.psum_pool(name="ps", bufs=1))
+        ctx.enter_context(tc.manual_schedule())
+
+        def tile(name, shape, dtype):
+            return sb.tile(shape, dtype, name=name, align_bytes=64)
+
+        def tiles(name, count, shape, dtype):
+            return [tile("%s%d" % (name, i), shape, dtype) for i in range(count)]
+
+        banks = [ps.tile([P, 512], F32, name="bank%d" % i) for i in range(8)]
+        ident = tile("ident", [P, P], F32)
+        ident_bf = tile("ident_bf", [P, P], BF16)
+        rows = tile("rows", [P, 640], BF16)
+        omega_words = tile("omega_words", [P, GROUPS, 2], F32)
+        vecs = tile("vecs", [P, 20], F32)
+        neg_rv = tile("neg_rv", [P, 8], F32)
+        warm = tile("warm", [P, 8], F32)
+        xs = tiles("xs", GROUPS, [P, 4096], BF16)
+        zs = tiles("zs", GROUPS, [P, 4096], BF16)
+        raw = tiles("raw", 3, [P, 4096], BF16)
+        stage = tiles("stage", NIL, [P, 2048], BF16)
+        turned = tiles("turned", 4, [P, 512], F32)
+        t_codes = tiles("t_codes", 4, [P, 1024], U32)
+        t_scales = tiles("t_scales", 4, [P, 1024], U8)
+        w_codes = tiles("w_codes", 2, [P, 1024], U32)
+        w_scales = tiles("w_scales", 2, [P, 1024], U8)
+        h_t = tiles("h_t", NH, [P, 512], F32)
+        h_sq = tiles("h_sq", 2, [P, 512], F32)
+        mid = tiles("mid", 4, [P, 512], BF16)
+        m_codes = tiles("m_codes", 2 * GROUPS, [P, 512], U32)
+        m_scales = tiles("m_scales", 2 * GROUPS, [P, 512], U8)
+        s_codes = tiles("s_codes", 4 * GROUPS, [P, 512], U32)
+        s_scales = tiles("s_scales", 4 * GROUPS, [P, 512], U8)
+        omega_bf = omega_words[:].rearrange("p g u -> p (g u)").bitcast(BF16)
+
+        def quantize(codes, scales, src):
+            nc.vector.quantize_mx(out=codes.bitcast(FP8X4), scales=scales, in_=src)
+
+        def cols(i, width=P):
+            return slice(i * width, (i + 1) * width)
+
+        def load_group(dst, src, g, first=0, last=4096):
+            view = src[cols(g, 512), :].rearrange("(p j) d -> p (j d)", j=4)
+            nc.sync.dma_start(out=dst[:, first:last], in_=view[:, first:last])
+
+        def load_weight(dst, src):
+            for kk in range(2):
+                view = src[cols(kk, 512), :].rearrange("(p t) r -> p (t r)", t=4)
+                nc.sync.dma_start(out=dst[:, cols(kk, 2048)], in_=view)
+
+        stage_of = {}
+
+        def staged(key):
+            return stage[stage_of.setdefault(key, len(stage_of) % NIL)]
+
+        def interleave(engine, dst, src):
+            out = dst.rearrange("p (c i t) -> p c t i", i=4, t=4)
+            in_ = src.rearrange("p t (c i) -> p c t i", i=4)
+            if engine == "V":
+                nc.vector.tensor_copy(out=out, in_=in_)
+            else:
+                nc.scalar.copy(out=out, in_=in_)
+
+        nc.vector.memset(rows[:], 0.0)
+        nc.vector.memset(warm[:], 0.0)
+        make_identity(nc, ident[:])
+        make_identity(nc, ident_bf[:])
+        nc.scalar.activation(out=warm[:], in_=warm[:], func=ACT.Tanh)
+
+        load_group(xs[0], x, 0, 0, 2048)
+        nc.sync.dma_start(out=rows[0:4, 0:512], in_=omega.rearrange("(g s) -> g s", g=4))
+        nc.sync.dma_start(out=rows[0:4, 512:640], in_=a.rearrange("(t r) -> t r", t=4))
+        nc.sync.dma_start(out=rows[4:12, 512:640], in_=rv.rearrange("(t r) -> t r", t=8))
+        nc.sync.dma_start(out=rows[12:20, 512:640], in_=ru.rearrange("(t r) -> t r", t=8))
+        load_group(xs[0], x, 0, 2048, 4096)
+        load_weight(raw[0], v)
+        dy_slot = [1, 0, 1, 2]
+
+        def load_product(g):
+            for h in range(2):
+                load_group(zs[g], x0, g, 2048 * h, 2048 * (h + 1))
+                load_group(raw[dy_slot[g]], dy, g, 2048 * h, 2048 * (h + 1))
+
+        load_product(0)
+        load_group(xs[1], x, 1)
+        load_weight(raw[2], um)
+
+        def small_vectors():
+            bank = banks[6]
+            words = rows[:, 0:512].bitcast(F32)
+            for u in range(2):
+                nc.tensor.transpose(bank[:, cols(u)], words[:, u:256:2], ident[:])
+            bank_bf = bank[:].bitcast(BF16)
+            nc.tensor.transpose(bank_bf[:, 512:640], rows[:, 512:640], ident_bf[:])
+            nc.vector.tensor_copy(out=omega_words[:], in_=bank[:, 0:256].rearrange("p (u g) -> p g u", u=2)[:, 0:4, :])
+            nc.vector.tensor_copy(out=vecs[:], in_=bank_bf[:, 512:532])
+            nc.vector.tensor_scalar(out=neg_rv[:], in0=vecs[:, 4:12], scalar1=-1.0, scalar2=None, op0=ALU.mult)
+
+        def weight_interleave(engine, w, kk):
+            src = raw[2 * w][:, cols(kk, 2048)].rearrange("p (t r) -> p t r", t=4)
+            interleave(engine, staged((w, kk))[:], src)
+
+        def weight_quantize(w, kk):
+            quantize(w_codes[w][:, cols(kk, 512)], w_scales[w][:, cols(kk, 512)], staged((w, kk))[:])
+
+        def pick(options, n):
+            return banks[options[n % len(options)]]
+
+        def turn(which, n, options=None):
+            g, j = divmod(n, 4)
+            words = (xs, zs)[which][g][:, cols(j, 1024)].bitcast(F32)
+            for kk in range(2):
+                for u in range(2):
+                    nc.tensor.transpose(pick(options or (XB, ZB)[which], n)[:, cols(2 * kk + u)], words[:, 256 * kk + u : 256 * (kk + 1) : 2], ident[:])
+
+        def turn_out(which, n, options=None):
+            out = turned[2 * which + n % 2][:].rearrange("p (k s u) -> p k s u", k=2, u=2)
+            nc.scalar.copy(out=out, in_=pick(options or (XB, ZB)[which], n)[:].rearrange("p (k u s) -> p k s u", k=2, u=2))
+
+        def turn_quantize(which, n):
+            g, j = divmod(n, 4)
+            i = 2 * which + g % 2
+            src = turned[2 * which + n % 2][:].bitcast(BF16)
+            if which == 0:
+                for kk in range(2):
+                    c = slice(512 * kk + P * j, 512 * kk + P * (j + 1))
+                    quantize(t_codes[i][:, c], t_scales[i][:, c], src[:, cols(kk, 512)])
+            else:
+                quantize(t_codes[i][:, cols(j, 256)], t_scales[i][:, cols(j, 256)], src)
+
+        made = []
+        weighed = []
+
+        def product(n):
+            made.append(n)
+            g, j = divmod(n, 4)
+            nc.vector.tensor_tensor(out=zs[g][:, cols(j, 1024)], in0=zs[g][:, cols(j, 1024)], in1=raw[dy_slot[g]][:, cols(j, 1024)], op=ALU.mult)
+
+        def weigh(n):
+            weighed.append(n)
+            g, j = divmod(n, 4)
+            nc.vector.tensor_scalar(out=xs[g][:, cols(j, 1024)], in0=xs[g][:, cols(j, 1024)], scalar1=omega_bf[:, n : n + 1], scalar2=None, op0=ALU.mult)
+
+        def pre(m, options=PB):
+            g, rt = divmod(m, 4)
+            i = g % 2
+            for kk in range(2):
+                w = slice(512 * kk + P * rt, 512 * kk + P * (rt + 1))
+                nc.tensor.matmul_mx(out=pick(options, m)[:], lhsT=w_codes[0][:, w].bitcast(FP8X4), lhsT_scale=w_scales[0][:, w],
+                                    rhs=t_codes[i][:, cols(kk, 512)].bitcast(FP8X4), rhs_scale=t_scales[i][:, cols(kk, 512)],
+                                    start=(kk == 0), stop=(kk == 1))
+
+        def tanh(m, options=PB):
+            rt = m % 4
+            nc.scalar.activation(out=h_t[m % NH][:], in_=pick(options, m)[:], func=ACT.Tanh, bias=vecs[:, rt : rt + 1])
+
+        def turn_h(m):
+            for j in range(4):
+                nc.tensor.transpose(pick(HB, m)[:, cols(j)], h_t[m % NH][:, cols(j)], ident[:])
+
+        def by_slot(bank):
+            return bank[:].rearrange("p (j r) -> p r j", j=4)
+
+        def square(m):
+            nc.scalar.activation(out=h_sq[m % 2][:].rearrange("p (r j) -> p r j", j=4), in_=by_slot(pick(HB, m)), func=ACT.Square)
+
+        def hw(m):
+            g = m // 4
+            out = mid[m % 2][:].rearrange("p (r j) -> p r j", j=4)
+            weights = omega_bf[:, 4 * g : 4 * g + 4].unsqueeze(1).to_broadcast([P, P, 4])
+            nc.vector.tensor_tensor(out=out, in0=by_slot(pick(HB, m)), in1=weights, op=ALU.mult)
+
+        def dh(m):
+            g, rt = divmod(m, 4)
+            i = 2 + g % 2
+            for j in range(4):
+                for kk in range(2):
+                    s = cols(2 * j + kk)
+                    w = slice(512 * kk + P * rt, 512 * kk + P * (rt + 1))
+                    nc.tensor.matmul_mx(out=pick(DB, m)[:, cols(j)], lhsT=t_codes[i][:, s].bitcast(FP8X4), lhsT_scale=t_scales[i][:, s],
+                                        rhs=w_codes[1][:, w].bitcast(FP8X4), rhs_scale=w_scales[1][:, w],
+                                        start=(kk == 0), stop=(kk == 1))
+
+        def dpre(m):
+            out = mid[2 + m % 2][:].rearrange("p (r j) -> p r j", j=4)
+            nc.vector.scalar_tensor_tensor(out=out, in0=h_sq[m % 2][:].rearrange("p (r j) -> p r j", j=4), scalar=1.0,
+                                           in1=by_slot(pick(DB, m)), op0=ALU.subtract, op1=ALU.mult)
+
+        def mid_quantize(which, m):
+            g, rt = divmod(m, 4)
+            i = GROUPS * which + g
+            quantize(m_codes[i][:, cols(rt)], m_scales[i][:, cols(rt)], mid[2 * which + m % 2][:])
+
+        pieces = [(0, 0, 0), (0, 1, 0), (1, 0, 0), (1, 1, 0), (1, 0, 1), (1, 0, 2), (1, 0, 3), (1, 1, 1), (1, 1, 2), (1, 1, 3)]
+        pieces += [(0, h, g) for h in range(2) for g in range(1, GROUPS)]
+
+        def piece_interleave(engine, f, first, count):
+            which, h, g = pieces[f]
+            c = slice(512 * h + P * first, 512 * h + P * (first + count))
+            src = (xs, zs)[which][g][:].rearrange("p (t d) -> p t d", t=4)[:, :, c]
+            interleave(engine, staged(f)[:, 512 * first : 512 * (first + count)], src)
+
+        def piece_index(which, h, g):
+            return 8 * which + 4 * h + g
+
+        def piece_quantize(f):
+            i = piece_index(*pieces[f])
+            quantize(s_codes[i][:], s_scales[i][:], staged(f)[:])
+
+        def gradient_pass(which, h, g):
+            i = piece_index(which, h, g)
+            m = GROUPS * (1 - which) + g
+            for dt in range(4):
+                nc.tensor.matmul_mx(out=banks[SWEEP_BANKS[h][dt]][:], lhsT=s_codes[i][:, cols(dt)].bitcast(FP8X4), lhsT_scale=s_scales[i][:, cols(dt)],
+                                    rhs=m_codes[m][:].bitcast(FP8X4), rhs_scale=m_scales[m][:],
+                                    start=(g == 0), stop=(g == GROUPS - 1))
+
+        def gradient_out(which, h, dt, engine):
+            t = 4 * h + dt
+            bank = banks[SWEEP_BANKS[h][dt]]
+            result = (raw + xs)[2 * which + h][:].bitcast(F32)[:, cols(dt, 512)]
+            scale = neg_rv[:, t : t + 1] if which == 0 else vecs[:, 12 + t : 13 + t]
+            if engine == "S":
+                nc.scalar.activation(out=result, in_=bank[:], func=ACT.Copy, scale=scale)
+            else:
+                nc.vector.tensor_scalar(out=result, in0=bank[:], scalar1=scale, scalar2=None, op0=ALU.mult)
+            nc.sync.dma_start(out=(out_0, out_1)[which][cols(t), :], in_=result)
+
+        quarters = [(f, i) for f in range(len(pieces)) for i in range(4)]
+        waiting = []
+
+        def fill(engine, count):
+            while count > 0 and quarters:
+                f, first = quarters[0]
+                take = min(count, 4 - first)
+                which, h, g = pieces[f]
+                if which == 1 and 4 * g + 3 not in made:
+                    return
+                assert which == 1 or 4 * g + 3 in weighed
+                piece_interleave(engine, f, first, take)
+                for i in range(take):
+                    quarters.pop(0)
+                count -= take
+                if first + take == 4:
+                    waiting.append(f)
+
+        def flush(keep=0):
+            while len(waiting) > keep:
+                piece_quantize(waiting.pop(0))
+
+        def inside(i):
+            return 0 <= i < 16
+
+        wide = (0, 7, 1, 4)
+        for n in range(4):
+            turn(0, n, wide)
+            turn_out(0, n, wide)
+            if n == 1:
+                small_vectors()
+            if n > 0:
+                turn_quantize(0, n - 1)
+            if n == 2:
+                weight_interleave("V", 0, 0)
+        turn_quantize(0, 3)
+        weight_interleave("S", 0, 1)
+        for n in range(4):
+            weigh(n)
+        fill("S", 4)
+        weight_quantize(0, 0)
+        load_product(1)
+        load_group(xs[2], x, 2)
+        product(0)
+        product(1)
+        weight_quantize(0, 1)
+        fill("V", 4)
+        product(2)
+        product(3)
+        load_product(2)
+        load_group(xs[3], x, 3)
+        flush()
+        for pair in range(2):
+            for n in (2 * pair, 2 * pair + 1):
+                turn(1, n, wide)
+                turn_out(1, n, wide)
+            for n in (2 * pair, 2 * pair + 1):
+                pre(n, (2, 3))
+                tanh(n, (2, 3))
+            for n in (2 * pair, 2 * pair + 1):
+                turn_quantize(1, n)
+            weight_interleave("V", 1, pair)
+        load_product(3)
+        turn(0, 4)
+        turn_out(0, 4)
+        fill("S", HEAD_S)
+        weight_quantize(1, 0)
+        product(4)
+        weight_quantize(1, 1)
+
+        sweeps = [(1, 0), (1, 1), (0, 0), (0, 1)]
+        passes = [(which, h, g) for which, h in sweeps for g in range(GROUPS)]
+        for m in range(17):
+            n = m + 4 + PL
+            z = m + 4
+            if inside(n - 1):
+                turn_quantize(0, n - 1)
+            if inside(z - 1) and m > 0:
+                turn_quantize(1, z - 1)
+            if inside(m - 1):
+                mid_quantize(0, m - 1)
+                mid_quantize(1, m - 1)
+            if inside(n):
+                turn(0, n)
+            if inside(z):
+                turn(1, z)
+            if inside(m):
+                turn_h(m)
+            if HEAD_PRE <= m + PL < 16:
+                pre(m + PL)
+            if inside(m):
+                dh(m)
+            if EARLY <= m < EARLY + 3:
+                assert pieces.index(passes[0]) not in waiting + [f for f, i in quarters]
+                gradient_pass(*passes.pop(0))
+            if inside(z + 1):
+                product(z + 1)
+            flush()
+            if inside(m + 4):
+                weigh(m + 4)
+            if inside(n):
+                turn_out(0, n)
+            if inside(z):
+                turn_out(1, z)
+            if inside(m):
+                square(m)
+            if HEAD_PRE <= m + PL < 16:
+                tanh(m + PL)
+            if m >= RAMP:
+                fill("V", V_RAMP)
+            fill("S", S_STEADY if m < RAMP else S_RAMP)
+            if inside(m):
+                hw(m)
+                dpre(m)
+
+        pending = []
+        for which, h, g in passes:
+            need = pieces.index((which, h, g))
+            fill("V", V_TAIL)
+            fill("S", S_TAIL)
+            while need in [f for f, i in quarters]:
+                fill("V", 1)
+            flush(0 if need in waiting or not quarters else 1)
+            if g == 0:
+                while len(pending) > 0 and pending[0][1] == h:
+                    gradient_out(*pending.pop(0), "S")
+            gradient_pass(which, h, g)
+            for engine in E_TAIL if quarters else "SV":
+                if pending:
+                    gradient_out(*pending.pop(0), engine)
+            if g == GROUPS - 1:
+                pending += [(which, h, dt) for dt in range(4)]
+        for i in range(len(pending)):
+            gradient_out(*pending[i], "SV"[i % 2])

@@ -16,25 +16,29 @@ ACT = mybir.ActivationFunctionType
 
 P = 128
 GROUPS = 4
-NH = 5
-NIL = 4
-XB = (0, 7)
-ZB = (1,)
-PB = (2,)
-HB = (3,)
-DB = (5, 6)
-SWEEP_BANKS = ((0, 7, 1, 4), (2, 3, 5, 6))
-S_STEADY = 1
-S_RAMP = 2
-V_RAMP = 0
-RAMP = 12
-EARLY = 13
-V_TAIL = 2
-S_TAIL = 1
-E_TAIL = "S"
-PL = 1
-HEAD_PRE = 4
-HEAD_S = 3
+PAIRS = 8
+LEAD = 3
+NH = 4
+NSQ = 6
+NT = 3
+NV = 2
+NS = 2
+UM_LATE = 0
+F_X = (4, 0, 0)
+F_XZ = (0, 2, 0)
+F_Z = (2, 4, 0)
+F_T = (4, 2, 0)
+UM_AT = 4
+FAST_FROM = 3
+ENG = "SSSSSSVSVSVSVVVVVVV"
+EV = "SSSSSSSSSSSSSSVS"
+GB = (2, 3, 0, 4, 5, 1, 6, 7)
+DU_BANKS = (2, 3)
+DV_BANKS = (0, 4, 5, 1, 2, 3, 6, 7)
+DU_PER = 6
+HELD = 4
+T_PER = 4
+E_T = "SS"
 
 
 def tile_low_rank_cross_gradients_f4_kernel(tc, x, x0, dy, v, um, a, omega, rv, ru, out_0, out_1):
@@ -42,7 +46,6 @@ def tile_low_rank_cross_gradients_f4_kernel(tc, x, x0, dy, v, um, a, omega, rv, 
     with ExitStack() as ctx:
         sb = ctx.enter_context(tc.tile_pool(name="sb", bufs=1))
         ps = ctx.enter_context(tc.psum_pool(name="ps", bufs=1))
-        ctx.enter_context(tc.manual_schedule())
 
         def tile(name, shape, dtype):
             return sb.tile(shape, dtype, name=name, align_bytes=64)
@@ -51,9 +54,12 @@ def tile_low_rank_cross_gradients_f4_kernel(tc, x, x0, dy, v, um, a, omega, rv, 
             return [tile("%s%d" % (name, i), shape, dtype) for i in range(count)]
 
         banks = [ps.tile([P, 512], F32, name="bank%d" % i) for i in range(8)]
+        turn_bank = banks[0:2]
+        pre_bank = banks[2:4]
+        h_bank = banks[4:6]
+        dh_bank = banks[6:8]
         ident = tile("ident", [P, P], F32)
         ident_bf = tile("ident_bf", [P, P], BF16)
-        rows = tile("rows", [P, 640], BF16)
         omega_words = tile("omega_words", [P, GROUPS, 2], F32)
         vecs = tile("vecs", [P, 20], F32)
         neg_rv = tile("neg_rv", [P, 8], F32)
@@ -61,19 +67,20 @@ def tile_low_rank_cross_gradients_f4_kernel(tc, x, x0, dy, v, um, a, omega, rv, 
         xs = tiles("xs", GROUPS, [P, 4096], BF16)
         zs = tiles("zs", GROUPS, [P, 4096], BF16)
         raw = tiles("raw", 3, [P, 4096], BF16)
-        stage = tiles("stage", NIL, [P, 2048], BF16)
-        turned = tiles("turned", 4, [P, 512], F32)
+        stage = {"V": tiles("stage_v", NV, [P, 2048], BF16), "S": tiles("stage_s", NS, [P, 2048], BF16)}
+        turned = tiles("turned", NT, [P, 1024], F32)
         t_codes = tiles("t_codes", 4, [P, 1024], U32)
         t_scales = tiles("t_scales", 4, [P, 1024], U8)
         w_codes = tiles("w_codes", 2, [P, 1024], U32)
         w_scales = tiles("w_scales", 2, [P, 1024], U8)
         h_t = tiles("h_t", NH, [P, 512], F32)
-        h_sq = tiles("h_sq", 2, [P, 512], F32)
-        mid = tiles("mid", 4, [P, 512], BF16)
+        h_sq = tiles("h_sq", NSQ, [P, 512], F32)
+        mid = tiles("mid", 2, [P, 1024], BF16)
         m_codes = tiles("m_codes", 2 * GROUPS, [P, 512], U32)
         m_scales = tiles("m_scales", 2 * GROUPS, [P, 512], U8)
         s_codes = tiles("s_codes", 4 * GROUPS, [P, 512], U32)
         s_scales = tiles("s_scales", 4 * GROUPS, [P, 512], U8)
+        rows = mid[1][:, 0:640]
         omega_bf = omega_words[:].rearrange("p g u -> p (g u)").bitcast(BF16)
 
         def quantize(codes, scales, src):
@@ -86,15 +93,28 @@ def tile_low_rank_cross_gradients_f4_kernel(tc, x, x0, dy, v, um, a, omega, rv, 
             view = src[cols(g, 512), :].rearrange("(p j) d -> p (j d)", j=4)
             nc.sync.dma_start(out=dst[:, first:last], in_=view[:, first:last])
 
-        def load_weight(dst, src):
-            for kk in range(2):
-                view = src[cols(kk, 512), :].rearrange("(p t) r -> p (t r)", t=4)
-                nc.sync.dma_start(out=dst[:, cols(kk, 2048)], in_=view)
+        def load_weight(dst, src, kk):
+            view = src[cols(kk, 512), :].rearrange("(p t) r -> p (t r)", t=4)
+            nc.sync.dma_start(out=dst[:, cols(kk, 2048)], in_=view)
+
+        dy_slot = [1, 0, 1, 2]
+
+        def load_product(g):
+            for h in range(2):
+                load_group(zs[g], x0, g, 2048 * h, 2048 * (h + 1))
+                load_group(raw[dy_slot[g]], dy, g, 2048 * h, 2048 * (h + 1))
 
         stage_of = {}
+        turned_of = {}
 
-        def staged(key):
-            return stage[stage_of.setdefault(key, len(stage_of) % NIL)]
+        def staged(key, engine=None):
+            if key not in stage_of:
+                used = [e for e, i in stage_of.values() if e == engine]
+                stage_of[key] = (engine, len(used) % len(stage[engine]))
+            return stage[stage_of[key][0]][stage_of[key][1]]
+
+        def turned_tile(key):
+            return turned[turned_of.setdefault(key, len(turned_of) % NT)]
 
         def interleave(engine, dst, src):
             out = dst.rearrange("p (c i t) -> p c t i", i=4, t=4)
@@ -104,32 +124,8 @@ def tile_low_rank_cross_gradients_f4_kernel(tc, x, x0, dy, v, um, a, omega, rv, 
             else:
                 nc.scalar.copy(out=out, in_=in_)
 
-        nc.vector.memset(rows[:], 0.0)
-        nc.vector.memset(warm[:], 0.0)
-        make_identity(nc, ident[:])
-        make_identity(nc, ident_bf[:])
-        nc.scalar.activation(out=warm[:], in_=warm[:], func=ACT.Tanh)
-
-        load_group(xs[0], x, 0, 0, 2048)
-        nc.sync.dma_start(out=rows[0:4, 0:512], in_=omega.rearrange("(g s) -> g s", g=4))
-        nc.sync.dma_start(out=rows[0:4, 512:640], in_=a.rearrange("(t r) -> t r", t=4))
-        nc.sync.dma_start(out=rows[4:12, 512:640], in_=rv.rearrange("(t r) -> t r", t=8))
-        nc.sync.dma_start(out=rows[12:20, 512:640], in_=ru.rearrange("(t r) -> t r", t=8))
-        load_group(xs[0], x, 0, 2048, 4096)
-        load_weight(raw[0], v)
-        dy_slot = [1, 0, 1, 2]
-
-        def load_product(g):
-            for h in range(2):
-                load_group(zs[g], x0, g, 2048 * h, 2048 * (h + 1))
-                load_group(raw[dy_slot[g]], dy, g, 2048 * h, 2048 * (h + 1))
-
-        load_product(0)
-        load_group(xs[1], x, 1)
-        load_weight(raw[2], um)
-
         def small_vectors():
-            bank = banks[6]
+            bank = banks[7]
             words = rows[:, 0:512].bitcast(F32)
             for u in range(2):
                 nc.tensor.transpose(bank[:, cols(u)], words[:, u:256:2], ident[:])
@@ -137,131 +133,114 @@ def tile_low_rank_cross_gradients_f4_kernel(tc, x, x0, dy, v, um, a, omega, rv, 
             nc.tensor.transpose(bank_bf[:, 512:640], rows[:, 512:640], ident_bf[:])
             nc.vector.tensor_copy(out=omega_words[:], in_=bank[:, 0:256].rearrange("p (u g) -> p g u", u=2)[:, 0:4, :])
             nc.vector.tensor_copy(out=vecs[:], in_=bank_bf[:, 512:532])
-            nc.vector.tensor_scalar(out=neg_rv[:], in0=vecs[:, 4:12], scalar1=-1.0, scalar2=None, op0=ALU.mult)
+            nc.vector.tensor_scalar(out=neg_rv[:], in0=bank_bf[:, 516:524], scalar1=-1.0, scalar2=None, op0=ALU.mult)
 
         def weight_interleave(engine, w, kk):
             src = raw[2 * w][:, cols(kk, 2048)].rearrange("p (t r) -> p t r", t=4)
-            interleave(engine, staged((w, kk))[:], src)
+            interleave(engine, staged((w, kk), engine)[:], src)
 
         def weight_quantize(w, kk):
             quantize(w_codes[w][:, cols(kk, 512)], w_scales[w][:, cols(kk, 512)], staged((w, kk))[:])
 
-        def pick(options, n):
-            return banks[options[n % len(options)]]
-
-        def turn(which, n, options=None):
+        def turn(which, n, bank):
             g, j = divmod(n, 4)
             words = (xs, zs)[which][g][:, cols(j, 1024)].bitcast(F32)
             for kk in range(2):
                 for u in range(2):
-                    nc.tensor.transpose(pick(options or (XB, ZB)[which], n)[:, cols(2 * kk + u)], words[:, 256 * kk + u : 256 * (kk + 1) : 2], ident[:])
+                    nc.tensor.transpose(bank[:, cols(2 * kk + u)], words[:, 256 * kk + u : 256 * (kk + 1) : 2], ident[:])
 
-        def turn_out(which, n, options=None):
-            out = turned[2 * which + n % 2][:].rearrange("p (k s u) -> p k s u", k=2, u=2)
-            nc.scalar.copy(out=out, in_=pick(options or (XB, ZB)[which], n)[:].rearrange("p (k u s) -> p k s u", k=2, u=2))
+        def turn_out(which, n, bank):
+            out = turned_tile((which, n // 2))[:].rearrange("p (k j s u) -> p k j s u", k=2, j=2, u=2)[:, :, n % 2, :, :]
+            nc.scalar.copy(out=out, in_=bank[:].rearrange("p (k u s) -> p k s u", k=2, u=2))
 
-        def turn_quantize(which, n):
-            g, j = divmod(n, 4)
+        def turn_quantize(which, pair):
+            g, half = divmod(pair, 2)
             i = 2 * which + g % 2
-            src = turned[2 * which + n % 2][:].bitcast(BF16)
-            if which == 0:
-                for kk in range(2):
-                    c = slice(512 * kk + P * j, 512 * kk + P * (j + 1))
-                    quantize(t_codes[i][:, c], t_scales[i][:, c], src[:, cols(kk, 512)])
-            else:
-                quantize(t_codes[i][:, cols(j, 256)], t_scales[i][:, cols(j, 256)], src)
+            quantize(t_codes[i][:, cols(half, 512)], t_scales[i][:, cols(half, 512)], turned_tile((which, pair))[:].bitcast(BF16))
 
         made = []
         weighed = []
 
-        def product(n):
-            made.append(n)
-            g, j = divmod(n, 4)
-            nc.vector.tensor_tensor(out=zs[g][:, cols(j, 1024)], in0=zs[g][:, cols(j, 1024)], in1=raw[dy_slot[g]][:, cols(j, 1024)], op=ALU.mult)
+        def product(pair):
+            made.append(pair)
+            g, half = divmod(pair, 2)
+            c = cols(half, 2048)
+            nc.vector.tensor_tensor(out=zs[g][:, c], in0=zs[g][:, c], in1=raw[dy_slot[g]][:, c], op=ALU.mult)
 
-        def weigh(n):
-            weighed.append(n)
-            g, j = divmod(n, 4)
-            nc.vector.tensor_scalar(out=xs[g][:, cols(j, 1024)], in0=xs[g][:, cols(j, 1024)], scalar1=omega_bf[:, n : n + 1], scalar2=None, op0=ALU.mult)
+        def weigh(pair):
+            weighed.append(pair)
+            for n in (2 * pair, 2 * pair + 1):
+                g, j = divmod(n, 4)
+                nc.vector.tensor_scalar(out=xs[g][:, cols(j, 1024)], in0=xs[g][:, cols(j, 1024)], scalar1=omega_bf[:, n : n + 1], scalar2=None, op0=ALU.mult)
 
-        def pre(m, options=PB):
+        def pre(m):
             g, rt = divmod(m, 4)
             i = g % 2
-            for kk in range(2):
-                w = slice(512 * kk + P * rt, 512 * kk + P * (rt + 1))
-                nc.tensor.matmul_mx(out=pick(options, m)[:], lhsT=w_codes[0][:, w].bitcast(FP8X4), lhsT_scale=w_scales[0][:, w],
-                                    rhs=t_codes[i][:, cols(kk, 512)].bitcast(FP8X4), rhs_scale=t_scales[i][:, cols(kk, 512)],
-                                    start=(kk == 0), stop=(kk == 1))
+            for half in range(2):
+                for kk in range(2):
+                    w = cols(4 * kk + rt)
+                    s = cols(2 * half + kk, 256)
+                    nc.tensor.matmul_mx(out=pre_bank[m % 2][:, cols(half, 256)], lhsT=w_codes[0][:, w].bitcast(FP8X4), lhsT_scale=w_scales[0][:, w],
+                                        rhs=t_codes[i][:, s].bitcast(FP8X4), rhs_scale=t_scales[i][:, s],
+                                        start=(kk == 0), stop=(kk == 1))
 
-        def tanh(m, options=PB):
+        def tanh(m):
             rt = m % 4
-            nc.scalar.activation(out=h_t[m % NH][:], in_=pick(options, m)[:], func=ACT.Tanh, bias=vecs[:, rt : rt + 1])
+            nc.scalar.activation(out=h_t[m % NH][:], in_=pre_bank[m % 2][:], func=ACT.Tanh, bias=vecs[:, rt : rt + 1])
 
         def turn_h(m):
             for j in range(4):
-                nc.tensor.transpose(pick(HB, m)[:, cols(j)], h_t[m % NH][:, cols(j)], ident[:])
+                nc.tensor.transpose(h_bank[m % 2][:, cols(j)], h_t[m % NH][:, cols(j)], ident[:])
 
         def by_slot(bank):
             return bank[:].rearrange("p (j r) -> p r j", j=4)
 
         def square(m):
-            nc.scalar.activation(out=h_sq[m % 2][:].rearrange("p (r j) -> p r j", j=4), in_=by_slot(pick(HB, m)), func=ACT.Square)
+            nc.scalar.activation(out=h_sq[m % NSQ][:].rearrange("p (r j) -> p r j", j=4), in_=by_slot(h_bank[m % 2]), func=ACT.Square)
 
         def hw(m):
             g = m // 4
-            out = mid[m % 2][:].rearrange("p (r j) -> p r j", j=4)
+            out = mid[0][:, cols(m % 2, 512)].rearrange("p (r j) -> p r j", j=4)
             weights = omega_bf[:, 4 * g : 4 * g + 4].unsqueeze(1).to_broadcast([P, P, 4])
-            nc.vector.tensor_tensor(out=out, in0=by_slot(pick(HB, m)), in1=weights, op=ALU.mult)
+            nc.vector.tensor_tensor(out=out, in0=by_slot(h_bank[m % 2]), in1=weights, op=ALU.mult)
 
         def dh(m):
             g, rt = divmod(m, 4)
             i = 2 + g % 2
             for j in range(4):
                 for kk in range(2):
-                    s = cols(2 * j + kk)
-                    w = slice(512 * kk + P * rt, 512 * kk + P * (rt + 1))
-                    nc.tensor.matmul_mx(out=pick(DB, m)[:, cols(j)], lhsT=t_codes[i][:, s].bitcast(FP8X4), lhsT_scale=t_scales[i][:, s],
+                    s = cols(4 * (j // 2) + 2 * kk + j % 2)
+                    w = cols(4 * kk + rt)
+                    nc.tensor.matmul_mx(out=dh_bank[m % 2][:, cols(j)], lhsT=t_codes[i][:, s].bitcast(FP8X4), lhsT_scale=t_scales[i][:, s],
                                         rhs=w_codes[1][:, w].bitcast(FP8X4), rhs_scale=w_scales[1][:, w],
                                         start=(kk == 0), stop=(kk == 1))
 
         def dpre(m):
-            out = mid[2 + m % 2][:].rearrange("p (r j) -> p r j", j=4)
-            nc.vector.scalar_tensor_tensor(out=out, in0=h_sq[m % 2][:].rearrange("p (r j) -> p r j", j=4), scalar=1.0,
-                                           in1=by_slot(pick(DB, m)), op0=ALU.subtract, op1=ALU.mult)
+            out = mid[1][:, cols(m % 2, 512)].rearrange("p (r j) -> p r j", j=4)
+            nc.vector.scalar_tensor_tensor(out=out, in0=h_sq[m % NSQ][:].rearrange("p (r j) -> p r j", j=4), scalar=1.0,
+                                           in1=by_slot(dh_bank[m % 2]), op0=ALU.subtract, op1=ALU.mult)
 
-        def mid_quantize(which, m):
-            g, rt = divmod(m, 4)
+        def mid_quantize(which, pair):
+            g, half = divmod(pair, 2)
             i = GROUPS * which + g
-            quantize(m_codes[i][:, cols(rt)], m_scales[i][:, cols(rt)], mid[2 * which + m % 2][:])
+            quantize(m_codes[i][:, cols(half, 256)], m_scales[i][:, cols(half, 256)], mid[which][:])
 
-        pieces = [(0, 0, 0), (0, 1, 0), (1, 0, 0), (1, 1, 0), (1, 0, 1), (1, 0, 2), (1, 0, 3), (1, 1, 1), (1, 1, 2), (1, 1, 3)]
-        pieces += [(0, h, g) for h in range(2) for g in range(1, GROUPS)]
+        ready = []
 
-        def piece_interleave(engine, f, first, count):
-            which, h, g = pieces[f]
-            c = slice(512 * h + P * first, 512 * h + P * (first + count))
-            src = (xs, zs)[which][g][:].rearrange("p (t d) -> p t d", t=4)[:, :, c]
-            interleave(engine, staged(f)[:, 512 * first : 512 * (first + count)], src)
+        def codes_of(which, c, g):
+            return 8 * which + 4 * (c // 2) + g, 256 * (c % 2)
 
-        def piece_index(which, h, g):
-            return 8 * which + 4 * h + g
-
-        def piece_quantize(f):
-            i = piece_index(*pieces[f])
-            quantize(s_codes[i][:], s_scales[i][:], staged(f)[:])
-
-        def gradient_pass(which, h, g):
-            i = piece_index(which, h, g)
+        def gradient_pass(which, t, g, bank):
+            assert (which, t // 2, g) in ready
+            i = codes_of(which, t // 2, g)[0]
             m = GROUPS * (1 - which) + g
-            for dt in range(4):
-                nc.tensor.matmul_mx(out=banks[SWEEP_BANKS[h][dt]][:], lhsT=s_codes[i][:, cols(dt)].bitcast(FP8X4), lhsT_scale=s_scales[i][:, cols(dt)],
-                                    rhs=m_codes[m][:].bitcast(FP8X4), rhs_scale=m_scales[m][:],
-                                    start=(g == 0), stop=(g == GROUPS - 1))
+            nc.tensor.matmul_mx(out=bank[:], lhsT=s_codes[i][:, cols(t % 4)].bitcast(FP8X4), lhsT_scale=s_scales[i][:, cols(t % 4)],
+                                rhs=m_codes[m][:].bitcast(FP8X4), rhs_scale=m_scales[m][:],
+                                start=(g == 0), stop=(g == GROUPS - 1))
 
-        def gradient_out(which, h, dt, engine):
-            t = 4 * h + dt
-            bank = banks[SWEEP_BANKS[h][dt]]
-            result = (raw + xs)[2 * which + h][:].bitcast(F32)[:, cols(dt, 512)]
+        def gradient_out(which, t, bank, engine):
+            h, dt = divmod(t, 4)
+            result = raw[(1, 2, 2, 0)[2 * which + h]][:].bitcast(F32)[:, cols(dt, 512)]
             scale = neg_rv[:, t : t + 1] if which == 0 else vecs[:, 12 + t : 13 + t]
             if engine == "S":
                 nc.scalar.activation(out=result, in_=bank[:], func=ACT.Copy, scale=scale)
@@ -269,137 +248,109 @@ def tile_low_rank_cross_gradients_f4_kernel(tc, x, x0, dy, v, um, a, omega, rv, 
                 nc.vector.tensor_scalar(out=result, in0=bank[:], scalar1=scale, scalar2=None, op0=ALU.mult)
             nc.sync.dma_start(out=(out_0, out_1)[which][cols(t), :], in_=result)
 
-        quarters = [(f, i) for f in range(len(pieces)) for i in range(4)]
-        waiting = []
-
-        def fill(engine, count):
-            while count > 0 and quarters:
-                f, first = quarters[0]
-                take = min(count, 4 - first)
-                which, h, g = pieces[f]
-                if which == 1 and 4 * g + 3 not in made:
-                    return
-                assert which == 1 or 4 * g + 3 in weighed
-                piece_interleave(engine, f, first, take)
-                for i in range(take):
-                    quarters.pop(0)
-                count -= take
-                if first + take == 4:
-                    waiting.append(f)
-
-        def flush(keep=0):
-            while len(waiting) > keep:
-                piece_quantize(waiting.pop(0))
-
         def inside(i):
-            return 0 <= i < 16
+            return 0 <= i < PAIRS
 
-        wide = (0, 7, 1, 4)
+        nc.vector.memset(rows, 0.0)
+        nc.vector.memset(warm[:], 0.0)
+        make_identity(nc, ident[:])
+        make_identity(nc, ident_bf[:])
+        nc.scalar.activation(out=warm[:], in_=warm[:], func=ACT.Tanh)
+        load_weight(raw[0], v, 0)
+        load_group(xs[0], x, 0, 0, 2048)
+        nc.sync.dma_start(out=rows[0:4, 0:512], in_=omega.rearrange("(g s) -> g s", g=4))
+        nc.sync.dma_start(out=rows[0:4, 512:640], in_=a.rearrange("(t r) -> t r", t=4))
+        nc.sync.dma_start(out=rows[4:12, 512:640], in_=rv.rearrange("(t r) -> t r", t=8))
+        nc.sync.dma_start(out=rows[12:20, 512:640], in_=ru.rearrange("(t r) -> t r", t=8))
+        load_weight(raw[0], v, 1)
+        load_group(xs[0], x, 0, 2048, 4096)
+        load_group(xs[1], x, 1)
+        if LEAD > 3:
+            load_group(xs[2], x, 2)
+        load_product(0)
+        if LEAD <= 3:
+            load_group(xs[2], x, 2)
+        load_weight(raw[2], um, 0)
+        load_weight(raw[2], um, 1)
+        weight_interleave("V", 0, 0)
+        weight_quantize(0, 0)
+        weight_interleave("V", 0, 1)
         for n in range(4):
-            turn(0, n, wide)
-            turn_out(0, n, wide)
+            turn(0, n, banks[n])
+            turn_out(0, n, banks[n])
             if n == 1:
                 small_vectors()
-            if n > 0:
-                turn_quantize(0, n - 1)
-            if n == 2:
-                weight_interleave("V", 0, 0)
-        turn_quantize(0, 3)
-        weight_interleave("S", 0, 1)
-        for n in range(4):
-            weigh(n)
-        fill("S", 4)
-        weight_quantize(0, 0)
-        load_product(1)
-        load_group(xs[2], x, 2)
-        product(0)
-        product(1)
-        weight_quantize(0, 1)
-        fill("V", 4)
-        product(2)
-        product(3)
-        load_product(2)
+                turn_quantize(0, 0)
+                weight_quantize(0, 1)
+        turn_quantize(0, 1)
         load_group(xs[3], x, 3)
-        flush()
-        for pair in range(2):
-            for n in (2 * pair, 2 * pair + 1):
-                turn(1, n, wide)
-                turn_out(1, n, wide)
-            for n in (2 * pair, 2 * pair + 1):
-                pre(n, (2, 3))
-                tanh(n, (2, 3))
-            for n in (2 * pair, 2 * pair + 1):
-                turn_quantize(1, n)
-            weight_interleave("V", 1, pair)
-        load_product(3)
-        turn(0, 4)
-        turn_out(0, 4)
-        fill("S", HEAD_S)
-        weight_quantize(1, 0)
-        product(4)
-        weight_quantize(1, 1)
+        load_product(1)
 
-        sweeps = [(1, 0), (1, 1), (0, 0), (0, 1)]
-        passes = [(which, h, g) for which, h in sweeps for g in range(GROUPS)]
-        for m in range(17):
-            n = m + 4 + PL
-            z = m + 4
-            if inside(n - 1):
-                turn_quantize(0, n - 1)
-            if inside(z - 1) and m > 0:
-                turn_quantize(1, z - 1)
-            if inside(m - 1):
-                mid_quantize(0, m - 1)
-                mid_quantize(1, m - 1)
-            if inside(n):
-                turn(0, n)
-            if inside(z):
-                turn(1, z)
-            if inside(m):
-                turn_h(m)
-            if HEAD_PRE <= m + PL < 16:
-                pre(m + PL)
-            if inside(m):
-                dh(m)
-            if EARLY <= m < EARLY + 3:
-                assert pieces.index(passes[0]) not in waiting + [f for f, i in quarters]
-                gradient_pass(*passes.pop(0))
-            if inside(z + 1):
-                product(z + 1)
-            flush()
-            if inside(m + 4):
-                weigh(m + 4)
-            if inside(n):
-                turn_out(0, n)
-            if inside(z):
-                turn_out(1, z)
-            if inside(m):
-                square(m)
-            if HEAD_PRE <= m + PL < 16:
-                tanh(m + PL)
-            if m >= RAMP:
-                fill("V", V_RAMP)
-            fill("S", S_STEADY if m < RAMP else S_RAMP)
-            if inside(m):
-                hw(m)
-                dpre(m)
+        with tc.manual_schedule(engines={mybir.EngineType.PE}):
+            for k in range(2, PAIRS + LEAD + 3):
+                z = k - LEAD
+                mx = k - 2
+                mz = z - 2
+                if k == UM_AT:
+                    weight_interleave("S", 1, 0)
+                    weight_interleave("V", 1, 1)
+                    load_product(3)
+                    weight_quantize(1, 0)
+                    weight_quantize(1, 1)
+                for e in range(2):
+                    if inside(k):
+                        turn(0, 2 * k + e, turn_bank[0])
+                        turn_out(0, 2 * k + e, turn_bank[0])
+                    if inside(z):
+                        turn(1, 2 * z + e, turn_bank[1])
+                        turn_out(1, 2 * z + e, turn_bank[1])
+                    if inside(mx - 1):
+                        turn_h(2 * mx - 2 + e)
+                        square(2 * mx - 2 + e)
+                    if inside(mx):
+                        pre(2 * mx + e)
+                        tanh(2 * mx + e)
+                    if inside(mz):
+                        dh(2 * mz + e)
+                    if inside(mx - 1):
+                        hw(2 * mx - 2 + e)
+                    if inside(mz):
+                        dpre(2 * mz + e)
+                if inside(k):
+                    turn_quantize(0, k)
+                if inside(z):
+                    turn_quantize(1, z)
+                for i in range(1 if z < FAST_FROM else 2):
+                    if z >= -1 and len(made) < PAIRS:
+                        product(len(made))
+                        if len(made) == 2:
+                            load_product(2)
+                if inside(mx - 1):
+                    mid_quantize(0, mx - 1)
+                if inside(mz):
+                    mid_quantize(1, mz)
 
-        pending = []
-        for which, h, g in passes:
-            need = pieces.index((which, h, g))
-            fill("V", V_TAIL)
-            fill("S", S_TAIL)
-            while need in [f for f, i in quarters]:
-                fill("V", 1)
-            flush(0 if need in waiting or not quarters else 1)
-            if g == 0:
-                while len(pending) > 0 and pending[0][1] == h:
-                    gradient_out(*pending.pop(0), "S")
-            gradient_pass(which, h, g)
-            for engine in E_TAIL if quarters else "SV":
-                if pending:
-                    gradient_out(*pending.pop(0), engine)
-            if g == GROUPS - 1:
-                pending += [(which, h, dt) for dt in range(4)]
-        for i in range(len(pending)):
-            gradient_out(*pending[i], "SV"[i % 2])
+        order = [(0, 0, 0), (0, 1, 0)] + [(1, h, g) for h in range(2) for g in range(GROUPS)]
+        order = order + [(0, h, g) for h in range(2) for g in range(1, GROUPS)]
+        jobs = [(which, 2 * h, 2, g) for which, h, g in order[:-3]] + [(0, c, 1, g) for c in (2, 3) for g in range(1, GROUPS)]
+        for i, (which, c, count, g) in enumerate(jobs):
+            if which == 0 and 2 * g not in weighed:
+                weigh(2 * g)
+                weigh(2 * g + 1)
+            engine = ENG[i]
+            dst = staged((which, c, g), engine)
+            for e in range(count):
+                src = (xs, zs)[which][g][:].rearrange("p (t d) -> p t d", t=4)[:, :, cols(c + e, 256)]
+                interleave(engine, dst[:, cols(e, 1024)], src)
+            j, first = codes_of(which, c, g)
+            with tc.high_priority():
+                quantize(s_codes[j][:, first : first + 256 * count], s_scales[j][:, first : first + 256 * count], dst[:, 0 : 1024 * count])
+            ready.extend([(which, c + e, g) for e in range(count)])
+
+        for which, first, count in ((1, 0, 4), (1, 4, 4), (0, 0, 4), (0, 4, 2), (0, 6, 2)):
+            for g in range(GROUPS):
+                for t in range(first, first + count):
+                    gradient_pass(which, t, g, banks[GB[t]])
+            for t in range(first, first + count):
+                with tc.high_priority():
+                    gradient_out(which, t, banks[GB[t]], EV[8 * (1 - which) + t])

@@ -21,6 +21,8 @@ LEAD = 3
 NH = 4
 NSQ = 6
 NT = 3
+PORD = "XPZHD"
+WARM = 2
 NV = 2
 NS = 2
 UM_LATE = 0
@@ -215,6 +217,11 @@ def tile_low_rank_cross_gradients_f4_kernel(tc, x, x0, dy, v, um, a, omega, rv, 
                                         rhs=w_codes[1][:, w].bitcast(FP8X4), rhs_scale=w_scales[1][:, w],
                                         start=(kk == 0), stop=(kk == 1))
 
+        def keep_warm(count):
+            for i in range(count):
+                nc.tensor.matmul_mx(out=dh_bank[0][:], lhsT=w_codes[0][:, 0:P].bitcast(FP8X4), lhsT_scale=w_scales[0][:, 0:P],
+                                    rhs=w_codes[0][:, 0:512].bitcast(FP8X4), rhs_scale=w_scales[0][:, 0:512], start=True, stop=True)
+
         def dpre(m):
             out = mid[1][:, cols(m % 2, 512)].rearrange("p (r j) -> p r j", j=4)
             nc.vector.scalar_tensor_tensor(out=out, in0=h_sq[m % NSQ][:].rearrange("p (r j) -> p r j", j=4), scalar=1.0,
@@ -298,20 +305,23 @@ def tile_low_rank_cross_gradients_f4_kernel(tc, x, x0, dy, v, um, a, omega, rv, 
                     weight_quantize(1, 0)
                     weight_quantize(1, 1)
                 for e in range(2):
-                    if inside(k):
-                        turn(0, 2 * k + e, turn_bank[0])
-                        turn_out(0, 2 * k + e, turn_bank[0])
-                    if inside(z):
-                        turn(1, 2 * z + e, turn_bank[1])
-                        turn_out(1, 2 * z + e, turn_bank[1])
-                    if inside(mx - 1):
-                        turn_h(2 * mx - 2 + e)
-                        square(2 * mx - 2 + e)
-                    if inside(mx):
-                        pre(2 * mx + e)
-                        tanh(2 * mx + e)
-                    if inside(mz):
-                        dh(2 * mz + e)
+                    for op in PORD:
+                        if op == "X" and inside(k):
+                            turn(0, 2 * k + e, turn_bank[0])
+                            turn_out(0, 2 * k + e, turn_bank[0])
+                        if op == "Z" and inside(z):
+                            turn(1, 2 * z + e, turn_bank[1])
+                            turn_out(1, 2 * z + e, turn_bank[1])
+                        if op == "H" and inside(mx - 1):
+                            turn_h(2 * mx - 2 + e)
+                            square(2 * mx - 2 + e)
+                        if op == "P" and inside(mx):
+                            pre(2 * mx + e)
+                            tanh(2 * mx + e)
+                        if op == "D" and inside(mz):
+                            dh(2 * mz + e)
+                        if op == "D" and mz < 0:
+                            keep_warm(WARM)
                     if inside(mx - 1):
                         hw(2 * mx - 2 + e)
                     if inside(mz):

@@ -18,11 +18,11 @@ P = 128
 GROUPS = 4
 PAIRS = 8
 LEAD = 3
-NH = 4
-NSQ = 6
+NH = 3
+NSQ = 5
 NT = 3
-PORD = "XPZHD"
-WARM = 2
+PORD = "XZHPD"
+WARM = 1
 NV = 2
 NS = 2
 UM_LATE = 0
@@ -32,7 +32,7 @@ F_Z = (2, 4, 0)
 F_T = (4, 2, 0)
 UM_AT = 4
 FAST_FROM = 3
-ENG = "SSSSSSVSVSVSVVVVVVV"
+ENG = "SVSSSSSVSVSVSSVSVVV"
 EV = "SSSSSSSSSSSSSSVS"
 GB = (2, 3, 0, 4, 5, 1, 6, 7)
 DU_BANKS = (2, 3)
@@ -63,11 +63,12 @@ def tile_low_rank_cross_gradients_f4_kernel(tc, x, x0, dy, v, um, a, omega, rv, 
         ident = tile("ident", [P, P], F32)
         ident_bf = tile("ident_bf", [P, P], BF16)
         omega_words = tile("omega_words", [P, GROUPS, 2], F32)
-        vecs = tile("vecs", [P, 20], F32)
+        vecs = tile("vecs", [P, 4], F32)
+        ru_f = tile("ru_f", [P, 8], F32)
         neg_rv = tile("neg_rv", [P, 8], F32)
         warm = tile("warm", [P, 8], F32)
         xs = tiles("xs", GROUPS, [P, 4096], BF16)
-        zs = tiles("zs", GROUPS, [P, 4096], BF16)
+        zs = tiles("zs", GROUPS + 1, [P, 4096], BF16)
         raw = tiles("raw", 3, [P, 4096], BF16)
         stage = {"V": tiles("stage_v", NV, [P, 2048], BF16), "S": tiles("stage_s", NS, [P, 2048], BF16)}
         turned = tiles("turned", NT, [P, 1024], F32)
@@ -103,7 +104,7 @@ def tile_low_rank_cross_gradients_f4_kernel(tc, x, x0, dy, v, um, a, omega, rv, 
 
         def load_product(g):
             for h in range(2):
-                load_group(zs[g], x0, g, 2048 * h, 2048 * (h + 1))
+                load_group(zs[g + 1], x0, g, 2048 * h, 2048 * (h + 1))
                 load_group(raw[dy_slot[g]], dy, g, 2048 * h, 2048 * (h + 1))
 
         stage_of = {}
@@ -118,9 +119,9 @@ def tile_low_rank_cross_gradients_f4_kernel(tc, x, x0, dy, v, um, a, omega, rv, 
         def turned_tile(key):
             return turned[turned_of.setdefault(key, len(turned_of) % NT)]
 
-        def interleave(engine, dst, src):
-            out = dst.rearrange("p (c i t) -> p c t i", i=4, t=4)
-            in_ = src.rearrange("p t (c i) -> p c t i", i=4)
+        def interleave(engine, dst, src, step=1):
+            out = dst.rearrange("p (e c i t) -> p e c t i", e=step, i=4, t=4)
+            in_ = src.rearrange("p t (c i e) -> p e c t i", e=step, i=4)
             if engine == "V":
                 nc.vector.tensor_copy(out=out, in_=in_)
             else:
@@ -134,7 +135,8 @@ def tile_low_rank_cross_gradients_f4_kernel(tc, x, x0, dy, v, um, a, omega, rv, 
             bank_bf = bank[:].bitcast(BF16)
             nc.tensor.transpose(bank_bf[:, 512:640], rows[:, 512:640], ident_bf[:])
             nc.vector.tensor_copy(out=omega_words[:], in_=bank[:, 0:256].rearrange("p (u g) -> p g u", u=2)[:, 0:4, :])
-            nc.vector.tensor_copy(out=vecs[:], in_=bank_bf[:, 512:532])
+            nc.vector.tensor_copy(out=vecs[:], in_=bank_bf[:, 512:516])
+            nc.vector.tensor_copy(out=ru_f[:].rearrange("p (k u e) -> p k u e", k=2, u=2), in_=bank_bf[:, 0:512].rearrange("p (u g e) -> p g u e", u=2, e=2)[:, 4:6])
             nc.vector.tensor_scalar(out=neg_rv[:], in0=bank_bf[:, 516:524], scalar1=-1.0, scalar2=None, op0=ALU.mult)
 
         def weight_interleave(engine, w, kk):
@@ -149,7 +151,8 @@ def tile_low_rank_cross_gradients_f4_kernel(tc, x, x0, dy, v, um, a, omega, rv, 
             words = (xs, zs)[which][g][:, cols(j, 1024)].bitcast(F32)
             for kk in range(2):
                 for u in range(2):
-                    nc.tensor.transpose(bank[:, cols(2 * kk + u)], words[:, 256 * kk + u : 256 * (kk + 1) : 2], ident[:])
+                    picked = words[:, 256 * kk + u : 256 * (kk + 1) : 2] if which == 0 else words[:, cols(2 * kk + u)]
+                    nc.tensor.transpose(bank[:, cols(2 * kk + u)], picked, ident[:])
 
         def turn_out(which, n, bank):
             out = turned_tile((which, n // 2))[:].rearrange("p (k j s u) -> p k j s u", k=2, j=2, u=2)[:, :, n % 2, :, :]
@@ -167,7 +170,9 @@ def tile_low_rank_cross_gradients_f4_kernel(tc, x, x0, dy, v, um, a, omega, rv, 
             made.append(pair)
             g, half = divmod(pair, 2)
             c = cols(half, 2048)
-            nc.vector.tensor_tensor(out=zs[g][:, c], in0=zs[g][:, c], in1=raw[dy_slot[g]][:, c], op=ALU.mult)
+            out = zs[g][:, c].rearrange("p (k u m e) -> p u k m e", k=4, u=2, e=2)
+            in0, in1 = (src[:, c].rearrange("p (k m u e) -> p u k m e", k=4, u=2, e=2) for src in (zs[g + 1], raw[dy_slot[g]]))
+            nc.vector.tensor_tensor(out=out, in0=in0, in1=in1, op=ALU.mult)
 
         def weigh(pair):
             weighed.append(pair)
@@ -248,12 +253,13 @@ def tile_low_rank_cross_gradients_f4_kernel(tc, x, x0, dy, v, um, a, omega, rv, 
         def gradient_out(which, t, bank, engine):
             h, dt = divmod(t, 4)
             result = raw[(1, 2, 2, 0)[2 * which + h]][:].bitcast(F32)[:, cols(dt, 512)]
-            scale = neg_rv[:, t : t + 1] if which == 0 else vecs[:, 12 + t : 13 + t]
+            scale = neg_rv[:, t : t + 1] if which == 0 else ru_f[:, t : t + 1]
             if engine == "S":
                 nc.scalar.activation(out=result, in_=bank[:], func=ACT.Copy, scale=scale)
             else:
                 nc.vector.tensor_scalar(out=result, in0=bank[:], scalar1=scale, scalar2=None, op0=ALU.mult)
-            nc.sync.dma_start(out=(out_0, out_1)[which][cols(t), :], in_=result)
+            dst = out_0[cols(t), :] if which == 0 else out_1.rearrange("(k m t) r -> k t m r", k=2, t=4)[h, dt]
+            nc.sync.dma_start(out=dst, in_=result)
 
         def inside(i):
             return 0 <= i < PAIRS
@@ -263,37 +269,38 @@ def tile_low_rank_cross_gradients_f4_kernel(tc, x, x0, dy, v, um, a, omega, rv, 
         make_identity(nc, ident[:])
         make_identity(nc, ident_bf[:])
         nc.scalar.activation(out=warm[:], in_=warm[:], func=ACT.Tanh)
-        load_weight(raw[0], v, 0)
-        load_group(xs[0], x, 0, 0, 2048)
-        nc.sync.dma_start(out=rows[0:4, 0:512], in_=omega.rearrange("(g s) -> g s", g=4))
-        nc.sync.dma_start(out=rows[0:4, 512:640], in_=a.rearrange("(t r) -> t r", t=4))
-        nc.sync.dma_start(out=rows[4:12, 512:640], in_=rv.rearrange("(t r) -> t r", t=8))
-        nc.sync.dma_start(out=rows[12:20, 512:640], in_=ru.rearrange("(t r) -> t r", t=8))
-        load_weight(raw[0], v, 1)
-        load_group(xs[0], x, 0, 2048, 4096)
-        load_group(xs[1], x, 1)
-        if LEAD > 3:
-            load_group(xs[2], x, 2)
-        load_product(0)
-        if LEAD <= 3:
-            load_group(xs[2], x, 2)
-        load_weight(raw[2], um, 0)
-        load_weight(raw[2], um, 1)
-        weight_interleave("V", 0, 0)
-        weight_quantize(0, 0)
-        weight_interleave("V", 0, 1)
-        for n in range(4):
-            turn(0, n, banks[n])
-            turn_out(0, n, banks[n])
-            if n == 1:
-                small_vectors()
-                turn_quantize(0, 0)
-                weight_quantize(0, 1)
-        turn_quantize(0, 1)
-        load_group(xs[3], x, 3)
-        load_product(1)
+        with tc.manual_schedule(engines={mybir.EngineType.PE, mybir.EngineType.SP}):
+            load_weight(raw[0], v, 0)
+            load_group(xs[0], x, 0, 0, 1024)
+            load_group(xs[0], x, 0, 1024, 2048)
+            nc.sync.dma_start(out=rows[0:4, 0:512], in_=omega.rearrange("(g s) -> g s", g=4))
+            nc.sync.dma_start(out=rows[0:4, 512:640], in_=a.rearrange("(t r) -> t r", t=4))
+            nc.sync.dma_start(out=rows[4:12, 512:640], in_=rv.rearrange("(t r) -> t r", t=8))
+            nc.sync.dma_start(out=rows[4:6, 0:512], in_=ru.rearrange("(k s) -> k s", k=2))
+            load_weight(raw[0], v, 1)
+            load_group(xs[0], x, 0, 2048, 4096)
+            load_group(xs[1], x, 1)
+            if LEAD > 3:
+                load_group(xs[2], x, 2)
+            load_product(0)
+            if LEAD <= 3:
+                load_group(xs[2], x, 2)
+            load_weight(raw[2], um, 0)
+            load_weight(raw[2], um, 1)
+            weight_interleave("V", 0, 0)
+            weight_quantize(0, 0)
+            weight_interleave("V", 0, 1)
+            for n in range(4):
+                turn(0, n, banks[n])
+                turn_out(0, n, banks[n])
+                if n == 1:
+                    small_vectors()
+                    turn_quantize(0, 0)
+                    weight_quantize(0, 1)
+            turn_quantize(0, 1)
+            load_group(xs[3], x, 3)
+            load_product(1)
 
-        with tc.manual_schedule(engines={mybir.EngineType.PE}):
             for k in range(2, PAIRS + LEAD + 3):
                 z = k - LEAD
                 mx = k - 2
@@ -343,6 +350,13 @@ def tile_low_rank_cross_gradients_f4_kernel(tc, x, x0, dy, v, um, a, omega, rv, 
         order = [(0, 0, 0), (0, 1, 0)] + [(1, h, g) for h in range(2) for g in range(GROUPS)]
         order = order + [(0, h, g) for h in range(2) for g in range(1, GROUPS)]
         jobs = [(which, 2 * h, 2, g) for which, h, g in order[:-3]] + [(0, c, 1, g) for c in (2, 3) for g in range(1, GROUPS)]
+
+        def job_quantize(which, c, count, g):
+            j, first = codes_of(which, c, g)
+            words = slice(first, first + 256 * count)
+            quantize(s_codes[j][:, words], s_scales[j][:, words], staged((which, c, g))[:, 0 : 1024 * count])
+
+        late = []
         for i, (which, c, count, g) in enumerate(jobs):
             if which == 0 and 2 * g not in weighed:
                 weigh(2 * g)
@@ -351,11 +365,17 @@ def tile_low_rank_cross_gradients_f4_kernel(tc, x, x0, dy, v, um, a, omega, rv, 
             dst = staged((which, c, g), engine)
             for e in range(count):
                 src = (xs, zs)[which][g][:].rearrange("p (t d) -> p t d", t=4)[:, :, cols(c + e, 256)]
-                interleave(engine, dst[:, cols(e, 1024)], src)
-            j, first = codes_of(which, c, g)
-            with tc.high_priority():
-                quantize(s_codes[j][:, first : first + 256 * count], s_scales[j][:, first : first + 256 * count], dst[:, 0 : 1024 * count])
+                interleave(engine, dst[:, cols(e, 1024)], src, 1 + which)
             ready.extend([(which, c + e, g) for e in range(count)])
+            if engine == "S":
+                with tc.high_priority():
+                    job_quantize(which, c, count, g)
+            else:
+                for job in late:
+                    job_quantize(*job)
+                late = [(which, c, count, g)]
+        for job in late:
+            job_quantize(*job)
 
         for which, first, count in ((1, 0, 4), (1, 4, 4), (0, 0, 4), (0, 4, 2), (0, 6, 2)):
             for g in range(GROUPS):

@@ -17,30 +17,17 @@ ACT = mybir.ActivationFunctionType
 P = 128
 GROUPS = 4
 PAIRS = 8
+X, Z = 0, 1
+HW, DPRE = 0, 1
 LEAD = 3
-NH = 3
-NSQ = 5
-NT = 3
-PORD = "XZHPD"
-WARM = 1
-NV = 2
-NS = 2
-UM_LATE = 0
-F_X = (4, 0, 0)
-F_XZ = (0, 2, 0)
-F_Z = (2, 4, 0)
-F_T = (4, 2, 0)
-UM_AT = 4
-FAST_FROM = 3
-ENG = "SVSSSSSVSVSVSSVSVVV"
-EV = "SSSSSSSSSSSSSSVS"
-GB = (2, 3, 0, 4, 5, 1, 6, 7)
-DU_BANKS = (2, 3)
-DV_BANKS = (0, 4, 5, 1, 2, 3, 6, 7)
-DU_PER = 6
-HELD = 4
-T_PER = 4
-E_T = "SS"
+UM_STEP = LEAD + 1
+DOUBLE_FROM = 3
+SCALAR_FIRST = 6
+VECTOR_LAST = 3
+H_BUFS = 4
+SQUARE_BUFS = 6
+TURNED_BUFS = 3
+STAGE_BUFS = 2
 
 
 def tile_low_rank_cross_gradients_f4_kernel(tc, x, x0, dy, v, um, a, omega, rv, ru, out_0, out_1):
@@ -63,31 +50,37 @@ def tile_low_rank_cross_gradients_f4_kernel(tc, x, x0, dy, v, um, a, omega, rv, 
         ident = tile("ident", [P, P], F32)
         ident_bf = tile("ident_bf", [P, P], BF16)
         omega_words = tile("omega_words", [P, GROUPS, 2], F32)
-        vecs = tile("vecs", [P, 4], F32)
-        ru_f = tile("ru_f", [P, 8], F32)
+        vecs = tile("vecs", [P, 20], F32)
         neg_rv = tile("neg_rv", [P, 8], F32)
         warm = tile("warm", [P, 8], F32)
         xs = tiles("xs", GROUPS, [P, 4096], BF16)
-        zs = tiles("zs", GROUPS + 1, [P, 4096], BF16)
+        zs = tiles("zs", GROUPS, [P, 4096], BF16)
         raw = tiles("raw", 3, [P, 4096], BF16)
-        stage = {"V": tiles("stage_v", NV, [P, 2048], BF16), "S": tiles("stage_s", NS, [P, 2048], BF16)}
-        turned = tiles("turned", NT, [P, 1024], F32)
+        stage = {"V": tiles("stage_v", STAGE_BUFS, [P, 2048], BF16), "S": tiles("stage_s", STAGE_BUFS, [P, 2048], BF16)}
+        turned = tiles("turned", TURNED_BUFS, [P, 1024], F32)
         t_codes = tiles("t_codes", 4, [P, 1024], U32)
         t_scales = tiles("t_scales", 4, [P, 1024], U8)
         w_codes = tiles("w_codes", 2, [P, 1024], U32)
         w_scales = tiles("w_scales", 2, [P, 1024], U8)
-        h_t = tiles("h_t", NH, [P, 512], F32)
-        h_sq = tiles("h_sq", NSQ, [P, 512], F32)
+        h_t = tiles("h_t", H_BUFS, [P, 512], F32)
+        h_sq = tiles("h_sq", SQUARE_BUFS, [P, 512], F32)
         mid = tiles("mid", 2, [P, 1024], BF16)
         m_codes = tiles("m_codes", 2 * GROUPS, [P, 512], U32)
         m_scales = tiles("m_scales", 2 * GROUPS, [P, 512], U8)
         s_codes = tiles("s_codes", 4 * GROUPS, [P, 512], U32)
         s_scales = tiles("s_scales", 4 * GROUPS, [P, 512], U8)
-        rows = mid[1][:, 0:640]
+        rows = mid[DPRE][:, 0:640]
         omega_bf = omega_words[:].rearrange("p g u -> p (g u)").bitcast(BF16)
+        large = (xs, zs)
+        dy_slot = [1, 0, 1, 2]
 
         def quantize(codes, scales, src):
             nc.vector.quantize_mx(out=codes.bitcast(FP8X4), scales=scales, in_=src)
+
+        def matmul(out, lhs, lhs_cols, rhs, rhs_cols, start, stop):
+            nc.tensor.matmul_mx(out=out, lhsT=lhs[0][:, lhs_cols].bitcast(FP8X4), lhsT_scale=lhs[1][:, lhs_cols],
+                                rhs=rhs[0][:, rhs_cols].bitcast(FP8X4), rhs_scale=rhs[1][:, rhs_cols],
+                                start=start, stop=stop)
 
         def cols(i, width=P):
             return slice(i * width, (i + 1) * width)
@@ -96,179 +89,160 @@ def tile_low_rank_cross_gradients_f4_kernel(tc, x, x0, dy, v, um, a, omega, rv, 
             view = src[cols(g, 512), :].rearrange("(p j) d -> p (j d)", j=4)
             nc.sync.dma_start(out=dst[:, first:last], in_=view[:, first:last])
 
-        def load_weight(dst, src, kk):
-            view = src[cols(kk, 512), :].rearrange("(p t) r -> p (t r)", t=4)
-            nc.sync.dma_start(out=dst[:, cols(kk, 2048)], in_=view)
+        def load_weight(dst, src, c):
+            view = src[cols(c, 512), :].rearrange("(p t) r -> p (t r)", t=4)
+            nc.sync.dma_start(out=dst[:, cols(c, 2048)], in_=view)
 
-        dy_slot = [1, 0, 1, 2]
-
-        def load_product(g):
-            for h in range(2):
-                load_group(zs[g + 1], x0, g, 2048 * h, 2048 * (h + 1))
-                load_group(raw[dy_slot[g]], dy, g, 2048 * h, 2048 * (h + 1))
+        def load_factors(g):
+            for half in range(2):
+                load_group(zs[g], x0, g, 2048 * half, 2048 * (half + 1))
+                load_group(raw[dy_slot[g]], dy, g, 2048 * half, 2048 * (half + 1))
 
         stage_of = {}
         turned_of = {}
 
         def staged(key, engine=None):
             if key not in stage_of:
-                used = [e for e, i in stage_of.values() if e == engine]
-                stage_of[key] = (engine, len(used) % len(stage[engine]))
+                earlier = [e for e, i in stage_of.values() if e == engine]
+                stage_of[key] = (engine, len(earlier) % STAGE_BUFS)
             return stage[stage_of[key][0]][stage_of[key][1]]
 
         def turned_tile(key):
-            return turned[turned_of.setdefault(key, len(turned_of) % NT)]
+            return turned[turned_of.setdefault(key, len(turned_of) % TURNED_BUFS)]
 
-        def interleave(engine, dst, src, step=1):
-            out = dst.rearrange("p (e c i t) -> p e c t i", e=step, i=4, t=4)
-            in_ = src.rearrange("p t (c i e) -> p e c t i", e=step, i=4)
+        def interleave(engine, dst, src):
+            out = dst.rearrange("p (c i t) -> p c t i", i=4, t=4)
+            in_ = src.rearrange("p t (c i) -> p c t i", i=4)
             if engine == "V":
                 nc.vector.tensor_copy(out=out, in_=in_)
             else:
                 nc.scalar.copy(out=out, in_=in_)
 
         def small_vectors():
-            bank = banks[7]
+            bank = dh_bank[1]
             words = rows[:, 0:512].bitcast(F32)
             for u in range(2):
                 nc.tensor.transpose(bank[:, cols(u)], words[:, u:256:2], ident[:])
             bank_bf = bank[:].bitcast(BF16)
             nc.tensor.transpose(bank_bf[:, 512:640], rows[:, 512:640], ident_bf[:])
-            nc.vector.tensor_copy(out=omega_words[:], in_=bank[:, 0:256].rearrange("p (u g) -> p g u", u=2)[:, 0:4, :])
-            nc.vector.tensor_copy(out=vecs[:], in_=bank_bf[:, 512:516])
-            nc.vector.tensor_copy(out=ru_f[:].rearrange("p (k u e) -> p k u e", k=2, u=2), in_=bank_bf[:, 0:512].rearrange("p (u g e) -> p g u e", u=2, e=2)[:, 4:6])
+            nc.vector.tensor_copy(out=omega_words[:], in_=bank[:, 0:256].rearrange("p (u g) -> p g u", u=2)[:, 0:GROUPS, :])
+            nc.vector.tensor_copy(out=vecs[:], in_=bank_bf[:, 512:532])
             nc.vector.tensor_scalar(out=neg_rv[:], in0=bank_bf[:, 516:524], scalar1=-1.0, scalar2=None, op0=ALU.mult)
 
-        def weight_interleave(engine, w, kk):
-            src = raw[2 * w][:, cols(kk, 2048)].rearrange("p (t r) -> p t r", t=4)
-            interleave(engine, staged((w, kk), engine)[:], src)
+        def weight_interleave(engine, w, c):
+            src = raw[2 * w][:, cols(c, 2048)].rearrange("p (t r) -> p t r", t=4)
+            interleave(engine, staged((w, c), engine)[:], src)
 
-        def weight_quantize(w, kk):
-            quantize(w_codes[w][:, cols(kk, 512)], w_scales[w][:, cols(kk, 512)], staged((w, kk))[:])
+        def weight_quantize(w, c):
+            quantize(w_codes[w][:, cols(c, 512)], w_scales[w][:, cols(c, 512)], staged((w, c))[:])
 
         def turn(which, n, bank):
             g, j = divmod(n, 4)
-            words = (xs, zs)[which][g][:, cols(j, 1024)].bitcast(F32)
-            for kk in range(2):
+            words = large[which][g][:, cols(j, 1024)].bitcast(F32)
+            for c in range(2):
                 for u in range(2):
-                    picked = words[:, 256 * kk + u : 256 * (kk + 1) : 2] if which == 0 else words[:, cols(2 * kk + u)]
-                    nc.tensor.transpose(bank[:, cols(2 * kk + u)], picked, ident[:])
+                    nc.tensor.transpose(bank[:, cols(2 * c + u)], words[:, 256 * c + u : 256 * (c + 1) : 2], ident[:])
+            out = turned_tile((which, n // 2))[:].rearrange("p (c j s u) -> p c j s u", c=2, j=2, u=2)[:, :, n % 2, :, :]
+            nc.scalar.copy(out=out, in_=bank[:].rearrange("p (c u s) -> p c s u", c=2, u=2))
 
-        def turn_out(which, n, bank):
-            out = turned_tile((which, n // 2))[:].rearrange("p (k j s u) -> p k j s u", k=2, j=2, u=2)[:, :, n % 2, :, :]
-            nc.scalar.copy(out=out, in_=bank[:].rearrange("p (k u s) -> p k s u", k=2, u=2))
+        def turned_operand(which, g):
+            i = 2 * which + g % 2
+            return t_codes[i], t_scales[i]
 
         def turn_quantize(which, pair):
             g, half = divmod(pair, 2)
-            i = 2 * which + g % 2
-            quantize(t_codes[i][:, cols(half, 512)], t_scales[i][:, cols(half, 512)], turned_tile((which, pair))[:].bitcast(BF16))
-
-        made = []
-        weighed = []
+            codes, scales = turned_operand(which, g)
+            quantize(codes[:, cols(half, 512)], scales[:, cols(half, 512)], turned_tile((which, pair))[:].bitcast(BF16))
 
         def product(pair):
-            made.append(pair)
             g, half = divmod(pair, 2)
             c = cols(half, 2048)
-            out = zs[g][:, c].rearrange("p (k u m e) -> p u k m e", k=4, u=2, e=2)
-            in0, in1 = (src[:, c].rearrange("p (k m u e) -> p u k m e", k=4, u=2, e=2) for src in (zs[g + 1], raw[dy_slot[g]]))
-            nc.vector.tensor_tensor(out=out, in0=in0, in1=in1, op=ALU.mult)
+            nc.vector.tensor_tensor(out=zs[g][:, c], in0=zs[g][:, c], in1=raw[dy_slot[g]][:, c], op=ALU.mult)
 
-        def weigh(pair):
-            weighed.append(pair)
-            for n in (2 * pair, 2 * pair + 1):
-                g, j = divmod(n, 4)
-                nc.vector.tensor_scalar(out=xs[g][:, cols(j, 1024)], in0=xs[g][:, cols(j, 1024)], scalar1=omega_bf[:, n : n + 1], scalar2=None, op0=ALU.mult)
-
-        def pre(m):
-            g, rt = divmod(m, 4)
-            i = g % 2
-            for half in range(2):
-                for kk in range(2):
-                    w = cols(4 * kk + rt)
-                    s = cols(2 * half + kk, 256)
-                    nc.tensor.matmul_mx(out=pre_bank[m % 2][:, cols(half, 256)], lhsT=w_codes[0][:, w].bitcast(FP8X4), lhsT_scale=w_scales[0][:, w],
-                                        rhs=t_codes[i][:, s].bitcast(FP8X4), rhs_scale=t_scales[i][:, s],
-                                        start=(kk == 0), stop=(kk == 1))
-
-        def tanh(m):
-            rt = m % 4
-            nc.scalar.activation(out=h_t[m % NH][:], in_=pre_bank[m % 2][:], func=ACT.Tanh, bias=vecs[:, rt : rt + 1])
-
-        def turn_h(m):
+        def weigh(g):
             for j in range(4):
-                nc.tensor.transpose(h_bank[m % 2][:, cols(j)], h_t[m % NH][:, cols(j)], ident[:])
+                n = 4 * g + j
+                nc.vector.tensor_scalar(out=xs[g][:, cols(j, 1024)], in0=xs[g][:, cols(j, 1024)],
+                                        scalar1=omega_bf[:, n : n + 1], scalar2=None, op0=ALU.mult)
+
+        def pre_and_tanh(m):
+            g, rt = divmod(m, 4)
+            bank = pre_bank[m % 2]
+            for half in range(2):
+                for c in range(2):
+                    matmul(bank[:, cols(half, 256)], (w_codes[0], w_scales[0]), cols(4 * c + rt),
+                           turned_operand(X, g), cols(2 * half + c, 256), c == 0, c == 1)
+            nc.scalar.activation(out=h_t[m % H_BUFS][:], in_=bank[:], func=ACT.Tanh, bias=vecs[:, rt : rt + 1])
 
         def by_slot(bank):
             return bank[:].rearrange("p (j r) -> p r j", j=4)
 
-        def square(m):
-            nc.scalar.activation(out=h_sq[m % NSQ][:].rearrange("p (r j) -> p r j", j=4), in_=by_slot(h_bank[m % 2]), func=ACT.Square)
+        def slot_last(ap):
+            return ap.rearrange("p (r j) -> p r j", j=4)
+
+        def turn_h_and_square(m):
+            for j in range(4):
+                nc.tensor.transpose(h_bank[m % 2][:, cols(j)], h_t[m % H_BUFS][:, cols(j)], ident[:])
+            nc.scalar.activation(out=slot_last(h_sq[m % SQUARE_BUFS][:]), in_=by_slot(h_bank[m % 2]), func=ACT.Square)
 
         def hw(m):
             g = m // 4
-            out = mid[0][:, cols(m % 2, 512)].rearrange("p (r j) -> p r j", j=4)
             weights = omega_bf[:, 4 * g : 4 * g + 4].unsqueeze(1).to_broadcast([P, P, 4])
-            nc.vector.tensor_tensor(out=out, in0=by_slot(h_bank[m % 2]), in1=weights, op=ALU.mult)
+            nc.vector.tensor_tensor(out=slot_last(mid[HW][:, cols(m % 2, 512)]), in0=by_slot(h_bank[m % 2]), in1=weights, op=ALU.mult)
 
         def dh(m):
             g, rt = divmod(m, 4)
-            i = 2 + g % 2
             for j in range(4):
-                for kk in range(2):
-                    s = cols(4 * (j // 2) + 2 * kk + j % 2)
-                    w = cols(4 * kk + rt)
-                    nc.tensor.matmul_mx(out=dh_bank[m % 2][:, cols(j)], lhsT=t_codes[i][:, s].bitcast(FP8X4), lhsT_scale=t_scales[i][:, s],
-                                        rhs=w_codes[1][:, w].bitcast(FP8X4), rhs_scale=w_scales[1][:, w],
-                                        start=(kk == 0), stop=(kk == 1))
-
-        def keep_warm(count):
-            for i in range(count):
-                nc.tensor.matmul_mx(out=dh_bank[0][:], lhsT=w_codes[0][:, 0:P].bitcast(FP8X4), lhsT_scale=w_scales[0][:, 0:P],
-                                    rhs=w_codes[0][:, 0:512].bitcast(FP8X4), rhs_scale=w_scales[0][:, 0:512], start=True, stop=True)
+                for c in range(2):
+                    matmul(dh_bank[m % 2][:, cols(j)], turned_operand(Z, g), cols(4 * (j // 2) + 2 * c + j % 2),
+                           (w_codes[1], w_scales[1]), cols(4 * c + rt), c == 0, c == 1)
 
         def dpre(m):
-            out = mid[1][:, cols(m % 2, 512)].rearrange("p (r j) -> p r j", j=4)
-            nc.vector.scalar_tensor_tensor(out=out, in0=h_sq[m % NSQ][:].rearrange("p (r j) -> p r j", j=4), scalar=1.0,
-                                           in1=by_slot(dh_bank[m % 2]), op0=ALU.subtract, op1=ALU.mult)
+            nc.vector.scalar_tensor_tensor(out=slot_last(mid[DPRE][:, cols(m % 2, 512)]), in0=slot_last(h_sq[m % SQUARE_BUFS][:]),
+                                           scalar=1.0, in1=by_slot(dh_bank[m % 2]), op0=ALU.subtract, op1=ALU.mult)
 
-        def mid_quantize(which, pair):
+        def mid_quantize(kind, pair):
             g, half = divmod(pair, 2)
-            i = GROUPS * which + g
-            quantize(m_codes[i][:, cols(half, 256)], m_scales[i][:, cols(half, 256)], mid[which][:])
+            i = GROUPS * kind + g
+            quantize(m_codes[i][:, cols(half, 256)], m_scales[i][:, cols(half, 256)], mid[kind][:])
 
-        ready = []
+        def sample_operand(which, h, g):
+            i = 2 * GROUPS * which + GROUPS * h + g
+            return s_codes[i], s_scales[i]
 
-        def codes_of(which, c, g):
-            return 8 * which + 4 * (c // 2) + g, 256 * (c % 2)
+        def job_interleave(engine, which, q, count, g):
+            dst = staged((which, q, g), engine)
+            for e in range(count):
+                src = large[which][g][:].rearrange("p (t d) -> p t d", t=4)[:, :, cols(q + e, 256)]
+                interleave(engine, dst[:, cols(e, 1024)], src)
+
+        def job_quantize(which, q, count, g):
+            codes, scales = sample_operand(which, q // 2, g)
+            words = slice(256 * (q % 2), 256 * (q % 2 + count))
+            quantize(codes[:, words], scales[:, words], staged((which, q, g))[:, 0 : 1024 * count])
 
         def gradient_pass(which, t, g, bank):
-            assert (which, t // 2, g) in ready
-            i = codes_of(which, t // 2, g)[0]
-            m = GROUPS * (1 - which) + g
-            nc.tensor.matmul_mx(out=bank[:], lhsT=s_codes[i][:, cols(t % 4)].bitcast(FP8X4), lhsT_scale=s_scales[i][:, cols(t % 4)],
-                                rhs=m_codes[m][:].bitcast(FP8X4), rhs_scale=m_scales[m][:],
-                                start=(g == 0), stop=(g == GROUPS - 1))
+            i = GROUPS * (DPRE if which == X else HW) + g
+            matmul(bank[:], sample_operand(which, t // 4, g), cols(t % 4), (m_codes[i], m_scales[i]), cols(0, 512),
+                   g == 0, g == GROUPS - 1)
 
-        def gradient_out(which, t, bank, engine):
-            h, dt = divmod(t, 4)
-            result = raw[(1, 2, 2, 0)[2 * which + h]][:].bitcast(F32)[:, cols(dt, 512)]
-            scale = neg_rv[:, t : t + 1] if which == 0 else ru_f[:, t : t + 1]
+        def gradient_out(which, t, bank, result, engine):
+            scale = neg_rv[:, t : t + 1] if which == X else vecs[:, 12 + t : 13 + t]
             if engine == "S":
                 nc.scalar.activation(out=result, in_=bank[:], func=ACT.Copy, scale=scale)
             else:
                 nc.vector.tensor_scalar(out=result, in0=bank[:], scalar1=scale, scalar2=None, op0=ALU.mult)
-            dst = out_0[cols(t), :] if which == 0 else out_1.rearrange("(k m t) r -> k t m r", k=2, t=4)[h, dt]
-            nc.sync.dma_start(out=dst, in_=result)
+            nc.sync.dma_start(out=(out_0, out_1)[which][cols(t), :], in_=result)
 
-        def inside(i):
-            return 0 <= i < PAIRS
+        def inside(pair):
+            return 0 <= pair < PAIRS
 
         nc.vector.memset(rows, 0.0)
         nc.vector.memset(warm[:], 0.0)
         make_identity(nc, ident[:])
         make_identity(nc, ident_bf[:])
         nc.scalar.activation(out=warm[:], in_=warm[:], func=ACT.Tanh)
+
         with tc.manual_schedule(engines={mybir.EngineType.PE, mybir.EngineType.SP}):
             load_weight(raw[0], v, 0)
             load_group(xs[0], x, 0, 0, 1024)
@@ -276,111 +250,101 @@ def tile_low_rank_cross_gradients_f4_kernel(tc, x, x0, dy, v, um, a, omega, rv, 
             nc.sync.dma_start(out=rows[0:4, 0:512], in_=omega.rearrange("(g s) -> g s", g=4))
             nc.sync.dma_start(out=rows[0:4, 512:640], in_=a.rearrange("(t r) -> t r", t=4))
             nc.sync.dma_start(out=rows[4:12, 512:640], in_=rv.rearrange("(t r) -> t r", t=8))
-            nc.sync.dma_start(out=rows[4:6, 0:512], in_=ru.rearrange("(k s) -> k s", k=2))
+            nc.sync.dma_start(out=rows[12:20, 512:640], in_=ru.rearrange("(t r) -> t r", t=8))
             load_weight(raw[0], v, 1)
             load_group(xs[0], x, 0, 2048, 4096)
             load_group(xs[1], x, 1)
-            if LEAD > 3:
-                load_group(xs[2], x, 2)
-            load_product(0)
-            if LEAD <= 3:
-                load_group(xs[2], x, 2)
+            load_factors(0)
+            load_group(xs[2], x, 2)
             load_weight(raw[2], um, 0)
             load_weight(raw[2], um, 1)
             weight_interleave("V", 0, 0)
             weight_quantize(0, 0)
             weight_interleave("V", 0, 1)
-            for n in range(4):
-                turn(0, n, banks[n])
-                turn_out(0, n, banks[n])
-                if n == 1:
-                    small_vectors()
-                    turn_quantize(0, 0)
-                    weight_quantize(0, 1)
-            turn_quantize(0, 1)
+            turn(X, 0, banks[0])
+            turn(X, 1, banks[1])
+            small_vectors()
+            turn_quantize(X, 0)
+            weight_quantize(0, 1)
+            turn(X, 2, banks[2])
+            turn(X, 3, banks[3])
+            turn_quantize(X, 1)
             load_group(xs[3], x, 3)
-            load_product(1)
+            load_factors(1)
 
-            for k in range(2, PAIRS + LEAD + 3):
-                z = k - LEAD
-                mx = k - 2
-                mz = z - 2
-                if k == UM_AT:
+            made = 0
+            for k in range(2, PAIRS + LEAD + 2):
+                z_pair = k - LEAD
+                pre_pair = k - 2
+                h_pair = pre_pair - 1
+                dh_pair = z_pair - 2
+                if k == UM_STEP:
                     weight_interleave("S", 1, 0)
                     weight_interleave("V", 1, 1)
-                    load_product(3)
+                    load_factors(3)
                     weight_quantize(1, 0)
                     weight_quantize(1, 1)
                 for e in range(2):
-                    for op in PORD:
-                        if op == "X" and inside(k):
-                            turn(0, 2 * k + e, turn_bank[0])
-                            turn_out(0, 2 * k + e, turn_bank[0])
-                        if op == "Z" and inside(z):
-                            turn(1, 2 * z + e, turn_bank[1])
-                            turn_out(1, 2 * z + e, turn_bank[1])
-                        if op == "H" and inside(mx - 1):
-                            turn_h(2 * mx - 2 + e)
-                            square(2 * mx - 2 + e)
-                        if op == "P" and inside(mx):
-                            pre(2 * mx + e)
-                            tanh(2 * mx + e)
-                        if op == "D" and inside(mz):
-                            dh(2 * mz + e)
-                        if op == "D" and mz < 0:
-                            keep_warm(WARM)
-                    if inside(mx - 1):
-                        hw(2 * mx - 2 + e)
-                    if inside(mz):
-                        dpre(2 * mz + e)
+                    if inside(k):
+                        turn(X, 2 * k + e, turn_bank[X])
+                    if inside(z_pair):
+                        turn(Z, 2 * z_pair + e, turn_bank[Z])
+                    if inside(h_pair):
+                        turn_h_and_square(2 * h_pair + e)
+                    if inside(pre_pair):
+                        pre_and_tanh(2 * pre_pair + e)
+                    if inside(dh_pair):
+                        dh(2 * dh_pair + e)
+                    if inside(h_pair):
+                        hw(2 * h_pair + e)
+                    if inside(dh_pair):
+                        dpre(2 * dh_pair + e)
                 if inside(k):
-                    turn_quantize(0, k)
-                if inside(z):
-                    turn_quantize(1, z)
-                for i in range(1 if z < FAST_FROM else 2):
-                    if z >= -1 and len(made) < PAIRS:
-                        product(len(made))
-                        if len(made) == 2:
-                            load_product(2)
-                if inside(mx - 1):
-                    mid_quantize(0, mx - 1)
-                if inside(mz):
-                    mid_quantize(1, mz)
+                    turn_quantize(X, k)
+                if inside(z_pair):
+                    turn_quantize(Z, z_pair)
+                for pair in range(made, min(PAIRS, made + (1 if z_pair < DOUBLE_FROM else 2))):
+                    product(pair)
+                    made = pair + 1
+                    if pair == 1:
+                        load_factors(2)
+                if inside(h_pair):
+                    mid_quantize(HW, h_pair)
+                if inside(dh_pair):
+                    mid_quantize(DPRE, dh_pair)
 
-        order = [(0, 0, 0), (0, 1, 0)] + [(1, h, g) for h in range(2) for g in range(GROUPS)]
-        order = order + [(0, h, g) for h in range(2) for g in range(1, GROUPS)]
-        jobs = [(which, 2 * h, 2, g) for which, h, g in order[:-3]] + [(0, c, 1, g) for c in (2, 3) for g in range(1, GROUPS)]
-
-        def job_quantize(which, c, count, g):
-            j, first = codes_of(which, c, g)
-            words = slice(first, first + 256 * count)
-            quantize(s_codes[j][:, words], s_scales[j][:, words], staged((which, c, g))[:, 0 : 1024 * count])
-
-        late = []
-        for i, (which, c, count, g) in enumerate(jobs):
-            if which == 0 and 2 * g not in weighed:
-                weigh(2 * g)
-                weigh(2 * g + 1)
-            engine = ENG[i]
-            dst = staged((which, c, g), engine)
-            for e in range(count):
-                src = (xs, zs)[which][g][:].rearrange("p (t d) -> p t d", t=4)[:, :, cols(c + e, 256)]
-                interleave(engine, dst[:, cols(e, 1024)], src, 1 + which)
-            ready.extend([(which, c + e, g) for e in range(count)])
-            if engine == "S":
+        jobs = [(X, 0, 2, 0), (X, 2, 2, 0)]
+        jobs += [(Z, q, 2, g) for q in (0, 2) for g in range(GROUPS)]
+        jobs += [(X, 0, 2, g) for g in range(1, GROUPS)]
+        jobs += [(X, q, 1, g) for q in (2, 3) for g in range(1, GROUPS)]
+        weighed = []
+        held = []
+        for i, job in enumerate(jobs):
+            which, g = job[0], job[3]
+            if which == X and g not in weighed:
+                weigh(g)
+                weighed.append(g)
+            if i < SCALAR_FIRST or (i % 2 == 1 and i < len(jobs) - VECTOR_LAST):
+                job_interleave("S", *job)
                 with tc.high_priority():
-                    job_quantize(which, c, count, g)
-            else:
-                for job in late:
                     job_quantize(*job)
-                late = [(which, c, count, g)]
-        for job in late:
-            job_quantize(*job)
+            else:
+                job_interleave("V", *job)
+                for earlier in held:
+                    job_quantize(*earlier)
+                held = [job]
+        for earlier in held:
+            job_quantize(*earlier)
 
-        for which, first, count in ((1, 0, 4), (1, 4, 4), (0, 0, 4), (0, 4, 2), (0, 6, 2)):
+        tile_bank = pre_bank + [turn_bank[X]] + h_bank + [turn_bank[Z]] + dh_bank
+        sweeps = ((Z, 0, 4), (Z, 4, 4), (X, 0, 4), (X, 4, 2), (X, 6, 2))
+        result_tile = {(Z, 0): raw[2], (Z, 1): raw[0], (X, 0): raw[1], (X, 1): raw[2]}
+        for which, first, count in sweeps:
             for g in range(GROUPS):
                 for t in range(first, first + count):
-                    gradient_pass(which, t, g, banks[GB[t]])
+                    gradient_pass(which, t, g, tile_bank[t])
             for t in range(first, first + count):
+                result = result_tile[which, t // 4][:].bitcast(F32)[:, cols(t % 4, 512)]
+                engine = "V" if (which, t) == (X, 6) else "S"
                 with tc.high_priority():
-                    gradient_out(which, t, banks[GB[t]], EV[8 * (1 - which) + t])
+                    gradient_out(which, t, tile_bank[t], result, engine)

from contextlib import ExitStack

import concourse.mybir as mybir
from concourse.masks import make_identity

B, D, R = 2048, 1024, 512
FLOPS = 4 * 2 * B * D * R

F32 = mybir.dt.float32
BF16 = mybir.dt.bfloat16
U32 = mybir.dt.uint32
U8 = mybir.dt.uint8
FP8X4 = mybir.dt.float8_e4m3fn_x4
ALU = mybir.AluOpType
ACT = mybir.ActivationFunctionType

P = 128
GROUPS = 4
PAIRS = 8
X, Z = 0, 1
HW, DPRE = 0, 1
LEAD = 3
UM_STEP = LEAD + 1
DOUBLE_FROM = 3
SCALAR_FIRST = 6
VECTOR_LAST = 3
H_BUFS = 4
SQUARE_BUFS = 6
TURNED_BUFS = 3
STAGE_BUFS = 2


def tile_low_rank_cross_gradients_f4_kernel(tc, x, x0, dy, v, um, a, omega, rv, ru, out_0, out_1):
    nc = tc.nc
    with ExitStack() as ctx:
        sb = ctx.enter_context(tc.tile_pool(name="sb", bufs=1))
        ps = ctx.enter_context(tc.psum_pool(name="ps", bufs=1))

        def tile(name, shape, dtype):
            return sb.tile(shape, dtype, name=name, align_bytes=64)

        def tiles(name, count, shape, dtype):
            return [tile("%s%d" % (name, i), shape, dtype) for i in range(count)]

        banks = [ps.tile([P, 512], F32, name="bank%d" % i) for i in range(8)]
        turn_bank = banks[0:2]
        pre_bank = banks[2:4]
        h_bank = banks[4:6]
        dh_bank = banks[6:8]
        ident = tile("ident", [P, P], F32)
        ident_bf = tile("ident_bf", [P, P], BF16)
        omega_words = tile("omega_words", [P, GROUPS, 2], F32)
        vecs = tile("vecs", [P, 20], F32)
        neg_rv = tile("neg_rv", [P, 8], F32)
        warm = tile("warm", [P, 8], F32)
        xs = tiles("xs", GROUPS, [P, 4096], BF16)
        zs = tiles("zs", GROUPS, [P, 4096], BF16)
        raw = tiles("raw", 3, [P, 4096], BF16)
        stage = {"V": tiles("stage_v", STAGE_BUFS, [P, 2048], BF16), "S": tiles("stage_s", STAGE_BUFS, [P, 2048], BF16)}
        turned = tiles("turned", TURNED_BUFS, [P, 1024], F32)
        t_codes = tiles("t_codes", 4, [P, 1024], U32)
        t_scales = tiles("t_scales", 4, [P, 1024], U8)
        w_codes = tiles("w_codes", 2, [P, 1024], U32)
        w_scales = tiles("w_scales", 2, [P, 1024], U8)
        h_t = tiles("h_t", H_BUFS, [P, 512], F32)
        h_sq = tiles("h_sq", SQUARE_BUFS, [P, 512], F32)
        mid = tiles("mid", 2, [P, 1024], BF16)
        m_codes = tiles("m_codes", 2 * GROUPS, [P, 512], U32)
        m_scales = tiles("m_scales", 2 * GROUPS, [P, 512], U8)
        s_codes = tiles("s_codes", 4 * GROUPS, [P, 512], U32)
        s_scales = tiles("s_scales", 4 * GROUPS, [P, 512], U8)
        rows = mid[DPRE][:, 0:640]
        omega_bf = omega_words[:].rearrange("p g u -> p (g u)").bitcast(BF16)
        large = (xs, zs)
        dy_slot = [1, 0, 1, 2]

        def quantize(codes, scales, src):
            nc.vector.quantize_mx(out=codes.bitcast(FP8X4), scales=scales, in_=src)

        def matmul(out, lhs, lhs_cols, rhs, rhs_cols, start, stop):
            nc.tensor.matmul_mx(out=out, lhsT=lhs[0][:, lhs_cols].bitcast(FP8X4), lhsT_scale=lhs[1][:, lhs_cols],
                                rhs=rhs[0][:, rhs_cols].bitcast(FP8X4), rhs_scale=rhs[1][:, rhs_cols],
                                start=start, stop=stop)

        def cols(i, width=P):
            return slice(i * width, (i + 1) * width)

        def load_group(dst, src, g, first=0, last=4096):
            view = src[cols(g, 512), :].rearrange("(p j) d -> p (j d)", j=4)
            nc.sync.dma_start(out=dst[:, first:last], in_=view[:, first:last])

        def load_weight(dst, src, c):
            view = src[cols(c, 512), :].rearrange("(p t) r -> p (t r)", t=4)
            nc.sync.dma_start(out=dst[:, cols(c, 2048)], in_=view)

        def load_factors(g):
            for half in range(2):
                load_group(zs[g], x0, g, 2048 * half, 2048 * (half + 1))
                load_group(raw[dy_slot[g]], dy, g, 2048 * half, 2048 * (half + 1))

        stage_of = {}
        turned_of = {}

        def staged(key, engine=None):
            if key not in stage_of:
                earlier = [e for e, i in stage_of.values() if e == engine]
                stage_of[key] = (engine, len(earlier) % STAGE_BUFS)
            return stage[stage_of[key][0]][stage_of[key][1]]

        def turned_tile(key):
            return turned[turned_of.setdefault(key, len(turned_of) % TURNED_BUFS)]

        def interleave(engine, dst, src):
            out = dst.rearrange("p (c i t) -> p c t i", i=4, t=4)
            in_ = src.rearrange("p t (c i) -> p c t i", i=4)
            if engine == "V":
                nc.vector.tensor_copy(out=out, in_=in_)
            else:
                nc.scalar.copy(out=out, in_=in_)

        def small_vectors():
            bank = dh_bank[1]
            words = rows[:, 0:512].bitcast(F32)
            for u in range(2):
                nc.tensor.transpose(bank[:, cols(u)], words[:, u:256:2], ident[:])
            bank_bf = bank[:].bitcast(BF16)
            nc.tensor.transpose(bank_bf[:, 512:640], rows[:, 512:640], ident_bf[:])
            nc.vector.tensor_copy(out=omega_words[:], in_=bank[:, 0:256].rearrange("p (u g) -> p g u", u=2)[:, 0:GROUPS, :])
            nc.vector.tensor_copy(out=vecs[:], in_=bank_bf[:, 512:532])
            nc.vector.tensor_scalar(out=neg_rv[:], in0=bank_bf[:, 516:524], scalar1=-1.0, scalar2=None, op0=ALU.mult)

        def weight_interleave(engine, w, c):
            src = raw[2 * w][:, cols(c, 2048)].rearrange("p (t r) -> p t r", t=4)
            interleave(engine, staged((w, c), engine)[:], src)

        def weight_quantize(w, c):
            quantize(w_codes[w][:, cols(c, 512)], w_scales[w][:, cols(c, 512)], staged((w, c))[:])

        def turn(which, n, bank):
            g, j = divmod(n, 4)
            words = large[which][g][:, cols(j, 1024)].bitcast(F32)
            for c in range(2):
                for u in range(2):
                    nc.tensor.transpose(bank[:, cols(2 * c + u)], words[:, 256 * c + u : 256 * (c + 1) : 2], ident[:])
            out = turned_tile((which, n // 2))[:].rearrange("p (c j s u) -> p c j s u", c=2, j=2, u=2)[:, :, n % 2, :, :]
            nc.scalar.copy(out=out, in_=bank[:].rearrange("p (c u s) -> p c s u", c=2, u=2))

        def turned_operand(which, g):
            i = 2 * which + g % 2
            return t_codes[i], t_scales[i]

        def turn_quantize(which, pair):
            g, half = divmod(pair, 2)
            codes, scales = turned_operand(which, g)
            quantize(codes[:, cols(half, 512)], scales[:, cols(half, 512)], turned_tile((which, pair))[:].bitcast(BF16))

        def product(pair):
            g, half = divmod(pair, 2)
            c = cols(half, 2048)
            nc.vector.tensor_tensor(out=zs[g][:, c], in0=zs[g][:, c], in1=raw[dy_slot[g]][:, c], op=ALU.mult)

        def weigh(g):
            for j in range(4):
                n = 4 * g + j
                nc.vector.tensor_scalar(out=xs[g][:, cols(j, 1024)], in0=xs[g][:, cols(j, 1024)],
                                        scalar1=omega_bf[:, n : n + 1], scalar2=None, op0=ALU.mult)

        def pre_and_tanh(m):
            g, rt = divmod(m, 4)
            bank = pre_bank[m % 2]
            for half in range(2):
                for c in range(2):
                    matmul(bank[:, cols(half, 256)], (w_codes[0], w_scales[0]), cols(4 * c + rt),
                           turned_operand(X, g), cols(2 * half + c, 256), c == 0, c == 1)
            nc.scalar.activation(out=h_t[m % H_BUFS][:], in_=bank[:], func=ACT.Tanh, bias=vecs[:, rt : rt + 1])

        def by_slot(bank):
            return bank[:].rearrange("p (j r) -> p r j", j=4)

        def slot_last(ap):
            return ap.rearrange("p (r j) -> p r j", j=4)

        def turn_h_and_square(m):
            for j in range(4):
                nc.tensor.transpose(h_bank[m % 2][:, cols(j)], h_t[m % H_BUFS][:, cols(j)], ident[:])
            nc.scalar.activation(out=slot_last(h_sq[m % SQUARE_BUFS][:]), in_=by_slot(h_bank[m % 2]), func=ACT.Square)

        def hw(m):
            g = m // 4
            weights = omega_bf[:, 4 * g : 4 * g + 4].unsqueeze(1).to_broadcast([P, P, 4])
            nc.vector.tensor_tensor(out=slot_last(mid[HW][:, cols(m % 2, 512)]), in0=by_slot(h_bank[m % 2]), in1=weights, op=ALU.mult)

        def dh(m):
            g, rt = divmod(m, 4)
            for j in range(4):
                for c in range(2):
                    matmul(dh_bank[m % 2][:, cols(j)], turned_operand(Z, g), cols(4 * (j // 2) + 2 * c + j % 2),
                           (w_codes[1], w_scales[1]), cols(4 * c + rt), c == 0, c == 1)

        def dpre(m):
            nc.vector.scalar_tensor_tensor(out=slot_last(mid[DPRE][:, cols(m % 2, 512)]), in0=slot_last(h_sq[m % SQUARE_BUFS][:]),
                                           scalar=1.0, in1=by_slot(dh_bank[m % 2]), op0=ALU.subtract, op1=ALU.mult)

        def mid_quantize(kind, pair):
            g, half = divmod(pair, 2)
            i = GROUPS * kind + g
            quantize(m_codes[i][:, cols(half, 256)], m_scales[i][:, cols(half, 256)], mid[kind][:])

        def sample_operand(which, h, g):
            i = 2 * GROUPS * which + GROUPS * h + g
            return s_codes[i], s_scales[i]

        def job_interleave(engine, which, q, count, g):
            dst = staged((which, q, g), engine)
            for e in range(count):
                src = large[which][g][:].rearrange("p (t d) -> p t d", t=4)[:, :, cols(q + e, 256)]
                interleave(engine, dst[:, cols(e, 1024)], src)

        def job_quantize(which, q, count, g):
            codes, scales = sample_operand(which, q // 2, g)
            words = slice(256 * (q % 2), 256 * (q % 2 + count))
            quantize(codes[:, words], scales[:, words], staged((which, q, g))[:, 0 : 1024 * count])

        def gradient_pass(which, t, g, bank):
            i = GROUPS * (DPRE if which == X else HW) + g
            matmul(bank[:], sample_operand(which, t // 4, g), cols(t % 4), (m_codes[i], m_scales[i]), cols(0, 512),
                   g == 0, g == GROUPS - 1)

        def gradient_out(which, t, bank, result, engine):
            scale = neg_rv[:, t : t + 1] if which == X else vecs[:, 12 + t : 13 + t]
            if engine == "S":
                nc.scalar.activation(out=result, in_=bank[:], func=ACT.Copy, scale=scale)
            else:
                nc.vector.tensor_scalar(out=result, in0=bank[:], scalar1=scale, scalar2=None, op0=ALU.mult)
            nc.sync.dma_start(out=(out_0, out_1)[which][cols(t), :], in_=result)

        def inside(pair):
            return 0 <= pair < PAIRS

        nc.vector.memset(rows, 0.0)
        nc.vector.memset(warm[:], 0.0)
        make_identity(nc, ident[:])
        make_identity(nc, ident_bf[:])
        nc.scalar.activation(out=warm[:], in_=warm[:], func=ACT.Tanh)

        with tc.manual_schedule(engines={mybir.EngineType.PE, mybir.EngineType.SP}):
            load_weight(raw[0], v, 0)
            load_group(xs[0], x, 0, 0, 1024)
            load_group(xs[0], x, 0, 1024, 2048)
            nc.sync.dma_start(out=rows[0:4, 0:512], in_=omega.rearrange("(g s) -> g s", g=4))
            nc.sync.dma_start(out=rows[0:4, 512:640], in_=a.rearrange("(t r) -> t r", t=4))
            nc.sync.dma_start(out=rows[4:12, 512:640], in_=rv.rearrange("(t r) -> t r", t=8))
            nc.sync.dma_start(out=rows[12:20, 512:640], in_=ru.rearrange("(t r) -> t r", t=8))
            load_weight(raw[0], v, 1)
            load_group(xs[0], x, 0, 2048, 4096)
            load_group(xs[1], x, 1)
            load_factors(0)
            load_group(xs[2], x, 2)
            load_weight(raw[2], um, 0)
            load_weight(raw[2], um, 1)
            weight_interleave("V", 0, 0)
            weight_quantize(0, 0)
            weight_interleave("V", 0, 1)
            turn(X, 0, banks[0])
            turn(X, 1, banks[1])
            small_vectors()
            turn_quantize(X, 0)
            weight_quantize(0, 1)
            turn(X, 2, banks[2])
            turn(X, 3, banks[3])
            turn_quantize(X, 1)
            load_group(xs[3], x, 3)
            load_factors(1)

            made = 0
            for k in range(2, PAIRS + LEAD + 2):
                z_pair = k - LEAD
                pre_pair = k - 2
                h_pair = pre_pair - 1
                dh_pair = z_pair - 2
                if k == UM_STEP:
                    weight_interleave("S", 1, 0)
                    weight_interleave("V", 1, 1)
                    load_factors(3)
                    weight_quantize(1, 0)
                    weight_quantize(1, 1)
                for e in range(2):
                    if inside(k):
                        turn(X, 2 * k + e, turn_bank[X])
                    if inside(z_pair):
                        turn(Z, 2 * z_pair + e, turn_bank[Z])
                    if inside(h_pair):
                        turn_h_and_square(2 * h_pair + e)
                    if inside(pre_pair):
                        pre_and_tanh(2 * pre_pair + e)
                    if inside(dh_pair):
                        dh(2 * dh_pair + e)
                    if inside(h_pair):
                        hw(2 * h_pair + e)
                    if inside(dh_pair):
                        dpre(2 * dh_pair + e)
                if inside(k):
                    turn_quantize(X, k)
                if inside(z_pair):
                    turn_quantize(Z, z_pair)
                for pair in range(made, min(PAIRS, made + (1 if z_pair < DOUBLE_FROM else 2))):
                    product(pair)
                    made = pair + 1
                    if pair == 1:
                        load_factors(2)
                if inside(h_pair):
                    mid_quantize(HW, h_pair)
                if inside(dh_pair):
                    mid_quantize(DPRE, dh_pair)

        jobs = [(X, 0, 2, 0), (X, 2, 2, 0)]
        jobs += [(Z, q, 2, g) for q in (0, 2) for g in range(GROUPS)]
        jobs += [(X, 0, 2, g) for g in range(1, GROUPS)]
        jobs += [(X, q, 1, g) for q in (2, 3) for g in range(1, GROUPS)]
        weighed = []
        held = []
        for i, job in enumerate(jobs):
            which, g = job[0], job[3]
            if which == X and g not in weighed:
                weigh(g)
                weighed.append(g)
            if i < SCALAR_FIRST or (i % 2 == 1 and i < len(jobs) - VECTOR_LAST):
                job_interleave("S", *job)
                with tc.high_priority():
                    job_quantize(*job)
            else:
                job_interleave("V", *job)
                for earlier in held:
                    job_quantize(*earlier)
                held = [job]
        for earlier in held:
            job_quantize(*earlier)

        tile_bank = pre_bank + [turn_bank[X]] + h_bank + [turn_bank[Z]] + dh_bank
        sweeps = ((Z, 0, 4), (Z, 4, 4), (X, 0, 4), (X, 4, 2), (X, 6, 2))
        result_tile = {(Z, 0): raw[2], (Z, 1): raw[0], (X, 0): raw[1], (X, 1): raw[2]}
        for which, first, count in sweeps:
            for g in range(GROUPS):
                for t in range(first, first + count):
                    gradient_pass(which, t, g, tile_bank[t])
            for t in range(first, first + count):
                result = result_tile[which, t // 4][:].bitcast(F32)[:, cols(t % 4, 512)]
                engine = "V" if (which, t) == (X, 6) else "S"
                with tc.high_priority():
                    gradient_out(which, t, tile_bank[t], result, engine)
